import numpy as np, ml_dtypes
CORES = [2,6,10,14,18,22,26,30]
N = 8
BF = ml_dtypes.bfloat16
def gentries(a):
    return np.ascontiguousarray(a.reshape(8, 16, -1).transpose(0, 2, 1)).reshape(8, -1)
def gtable(e):
    e = np.asarray(e); return np.ascontiguousarray(e.reshape(8, -1, 16).transpose(0, 2, 1)).reshape(128, -1).astype(np.int32)
S, G, CAP, WN, M, Q, RO, H, T0 = 3328, 112, 16, 144, 512, 4096, 3, 4, 192
W, L = S + (N - 1) * G, (N - 1) * CAP + WN
def lines(rng, n):
    base = rng.integers(0, 256, (N, 8, 1, n)); amp = rng.choice(np.array([0.0, 2.0, 12.0, 50.0]), (N, 8, 1, n))
    return np.clip(np.rint(base + amp * rng.standard_normal((N, 8, 15, n))), 0, 255).astype(np.int64)
def parts(rng):
    st = np.where(rng.random((N, 8, S)) < rng.choice(np.array([0.3, 0.45, 0.6]), (N, 8, 1)), -1, rng.integers(0, T0, (N, 8, S)))
    x = np.concatenate([lines(rng, S), st[:, :, None, :]], axis=2)
    order = np.argsort(st, axis=-1, kind="stable"); pos = np.argsort(order, axis=-1)
    span = rng.choice(np.array([4, 32, 300]), (N, 8, 1, S))
    at = np.clip(pos[:, :, None, :] + (span * (rng.random((N, 8, 16, S)) * 4 - 3)).astype(np.int64), 0, S - 1)
    nb = np.take_along_axis(order[:, :, None, :], at, 3)
    gh = rng.random((N, 8, 16, S)) < rng.choice(np.array([0.01, 0.03, 0.08]), (N, 8, 1, 1))
    nb = np.where(gh, rng.integers(S, W, (N, 8, 16, S)), nb)
    pl = np.concatenate([lines(rng, M), rng.integers(0, 256, (N, 8, 1, M))], axis=2); w = rng.integers(0, 256, (N, 8, 16, 1))
    none = np.sum(st < 0, axis=-1)[:, :, None]; k = np.minimum(none + (rng.random((N, 8, RO * WN)) * (S - none)).astype(np.int64), S - 1)
    wl = np.take_along_axis(order, k, 2); wl = np.where(rng.random(wl.shape) < 0.1, rng.integers(0, S, wl.shape), wl).reshape(N, 8, RO, WN)
    return x, nb, pl, w, wl, rng.integers(0, S, (N, 8, N - 1, G))
def pack(x, nb, pl, w, wl, sl):
    return {"x0": x.reshape(N, 128, S).astype(np.float32).astype(BF), "nb": np.ascontiguousarray(nb.reshape(N, 128, S)).astype(np.int32),
            "pull": pl.reshape(N, 128, M).astype(np.float32).astype(BF), "wt": w.reshape(N, 128, 1).astype(np.int32),
            "wants": np.stack([gtable(a.reshape(8, -1)) for a in wl]), "snd": np.stack([gtable(a.reshape(8, -1)) for a in sl])}
def aim(bl, lo):
    place = np.array([np.sum(bl[:i] == bl[i]) for i in range(len(bl))])
    return S + bl * G + lo + place % CAP
def brim(rng, x, nb, w, wl, sl, g):
    K = (N - 1) * CAP; w[:, g] = 0; w[:, g, 0] = 16; w[:, g, 1] = 1
    for r in range(N):
        zs = rng.permutation(Q); h = ((zs * zs >> 5) + 194) & (Q - 1)
        u, i = np.unique(np.where(h >= S, h - S, h), return_index=True)
        p = rng.permutation(np.nonzero(u)[0])[:L]; z = zs[i[p]]
        o = rng.permutation(np.setdiff1d(np.arange(1, S), u[p]))[:3 * WN + 2 * K]
        o[2 * WN + K + int(rng.integers(0, K))] = 0
        one, two, asked, late, last = np.split(o, [WN, 2 * WN, 2 * WN + K, 2 * WN + 2 * K])
        x[r, g, 15, u[p]] = -1
        for q, k in ((one, 0), (two, 0), (asked, 1), (late, 2)):
            x[r, g, 2, q] = 100 * k + rng.integers(0, 50, len(q)); x[r, g, 3, q] = 250 - 100 * k - rng.integers(0, 50, len(q))
            x[r, g, 15, q] = 60 * k + rng.integers(0, 50, len(q))
        end = np.concatenate([late, last]); x[r, g, 0, end] = z >> 4; x[r, g, 1, end] = z & 15
        x[r, g, 15, last] = rng.integers(0, T0, WN)
        nb[r, g][:, o] = o
        sl[r, g, :, :CAP] = asked.reshape(N - 1, CAP); sl[r, g, :, G - CAP:] = late.reshape(N - 1, CAP)
        bl = np.concatenate([rng.permutation(np.repeat(np.arange(N - 1), CAP)), rng.integers(0, N - 1, WN - K)])
        nb[r, g][rng.integers(0, 16, WN), one] = aim(bl, 0)
        b = int(rng.integers(0, N - 1)); bl = rng.permutation(np.arange(L - CAP) % (N - 2))
        bl = np.concatenate([bl + (bl >= b), np.full(CAP, b)])
        nb[r, g][rng.integers(0, 16, L), np.concatenate([asked, two])] = aim(bl, G - CAP)
        wl[r, g, 0] = one; wl[r, g, 1] = two; wl[r, g, 2] = last
def setup_inputs(rng):
    return pack(*parts(rng))
def setup_inputs_room(rng):
    x, nb, pl, w, wl, sl = parts(rng); k = S // 8
    for r in range(N):
        for g in range(8):
            o = rng.permutation(S); a, b, c, e = o[:k], o[k:2 * k], o[2 * k:3 * k], o[3 * k:]
            x[r, g, 15, a] = T0 - 1; x[r, g, 0, a] = 255; x[r, g, 1, a] = 0
            x[r, g, 15, b] = 0; x[r, g, 0, b] = rng.integers(0, 255, k); x[r, g, 1, b] = rng.integers(1, 256, k)
            x[r, g, 15, c] = rng.integers(0, T0, k); x[r, g, 15, e] = -1
            for q in (a[:k // 2], b, c): nb[r, g][:, q] = q
            sl[r, g] = a[rng.integers(0, k, (N - 1, G))]
            n = rng.choice(np.array([0, 1, CAP - 1, CAP, CAP + 1]), N - 1)
            if r == 0: n[0] = (CAP, CAP + 1, CAP - 1, 0, 1, CAP + 9, CAP, CAP + 1)[g]
            else: n[rng.integers(0, N - 1)] = CAP + 9
            to = np.concatenate([S + j * G + rng.integers(0, G, int(n[j])) for j in range(N - 1)])
            go = rng.permutation(b)[:len(to)]; nb[r, g][rng.integers(0, 16, len(to)), go] = to
            wl[r, g, 0] = rng.permutation(np.concatenate([go, rng.permutation(c)[:WN - len(to)]]))
    brim(rng, x, nb, w, wl, sl, 6)
    return pack(x, nb, pl, w, wl, sl)
def setup_inputs_ties(rng):
    x, nb, pl, w, wl, sl = parts(rng); n = (N, 8, 1, S); row = np.arange(15)[:, None]
    p = 100 + (row == rng.integers(0, 22, n)).astype(np.int64) - (row == rng.integers(0, 22, n)) + (rng.random(n) < 0.1)
    x = np.concatenate([p, rng.choice(np.array([-1, -1, -1, 0, 1, 2, T0 - 2, T0 - 1]), n)], axis=2); x[:, :, 15, ::S - 1] = 0
    wl[:, :, :, 0] = 0; wl[:, :, :, 1] = S - 1; nb[:, 1::2, 8:] = nb[:, 1::2, :8]
    return pack(x, nb, pl, w, wl, sl)
def setup_inputs_crowd(rng):
    x, nb, pl, w, wl, sl = parts(rng)
    x[:, :4, :15] = np.take_along_axis(x[:, :4, :15], rng.integers(0, 8, (N, 4, 1, S)), 3)
    nb = np.where(rng.random((N, 8, 1, S)) < 0.6, np.arange(S), nb)
    w[:, 5] = 0; x[:, 5, 15][:, 97 * np.arange(RO)] = -1
    ts, zs = np.nonzero((((np.arange(Q) ** 2 >> 5) + 97 * np.arange(RO)[:, None]) & (Q - 1)) == S)
    t = int(ts[0]); z = int(zs[rng.integers(0, int(np.sum(ts == t)))])
    w[:, 7] = 0; w[:, 7, 0] = z >> 4; w[:, 7, 1] = 1
    for r in range(N):
        for g in (0, 2, 4, 6):
            few = np.concatenate([np.array([0, S - 1]), rng.integers(0, S, 10)])
            x[r, g, 15, few] = T0 - 1; nb[r, g][:, few] = few; wl[r, g] = few[rng.integers(0, 12, (RO, WN))]
        half = 1 + rng.permutation(S - 1)[:S // 2]; few = half[:8]
        x[r, 7, 0, half] = 16; x[r, 7, 1, half] = z & 15; x[r, 7, 15, 0] = -1
        x[r, 7, 15, few] = T0 - 1; nb[r, 7][:, few] = few; wl[r, 7, t, :8] = few
    return pack(x, nb, pl, w, wl, sl)
def setup_inputs_bare(rng):
    x, nb, pl, w, wl, sl = parts(rng); q = rng.permutation(N); g = rng.permutation(8)
    x[:, g[0], 15] = -1; v = x[:, g[1], 15]; x[:, g[1], 15] = np.where(v < 0, rng.integers(0, T0, v.shape), v)
    nb[:, g[3]] = rng.choice(np.array([0, S - 1, S, W - 1]), (N, 16, S)); sl[:, g[2]] = rng.choice(np.array([0, S - 1, S // 2, 3]), (N, N - 1, G))
    nb[q[0]] = rng.integers(S, W, (8, 16, S)); nb[q[1]] = rng.integers(0, S, (8, 16, S))
    return pack(x, nb, pl, w, wl, sl)
def setup_inputs_spread(rng):
    x, nb, pl, w, wl, sl = parts(rng)
    p = np.minimum((np.exp2(8 * rng.random((N, 8, 1, S))) * rng.random((N, 8, 15, S))).astype(np.int64), 255)
    st = np.minimum(np.exp2(7.6 * rng.random((N, 8, 1, S))).astype(np.int64) - 1, T0 - 1)
    st = np.where(rng.random((N, 8, 1, S)) < rng.choice(np.array([0.1, 0.4, 0.8]), (N, 8, 1, 1)), -1, st)
    w = np.minimum(np.exp2(8 * rng.random((N, 8, 16, 1))).astype(np.int64), 255)
    pl = np.minimum((np.exp2(8 * rng.random((N, 8, 1, M))) * rng.random((N, 8, 16, M))).astype(np.int64), 255)
    nb = np.where(rng.random((N, 8, 1, S)) < 0.5, rng.integers(0, W, nb.shape), nb)
    return pack(np.concatenate([p, st], axis=2), nb, pl, w, rng.integers(0, S, wl.shape), sl)
def check_inputs(d):
    bad = []
    v = np.asarray(d["x0"]).astype(np.float32).reshape(N, 8, 16, S)
    for k, a, lo, hi in (("paths of x0", v[:, :, :15], 0, 255), ("stamps of x0", v[:, :, 15], -1, T0 - 1), ("pull", np.asarray(d["pull"]).astype(np.float32), 0, 255), ("wt", d["wt"], 0, 255),
                         ("nb", d["nb"], 0, W - 1), ("wants", d["wants"], 0, S - 1), ("snd", d["snd"], 0, S - 1)):
        if not np.all((a >= lo) & (a <= hi) & (a == np.floor(a))): bad.append("range of " + k)
    return bad
def reference(x0, nb, pull, wt, wants, snd):
    x = x0.astype(np.float32).astype(np.int64).reshape(N, 8, 16, S); nbr = nb.astype(np.int64).reshape(N, 8, 16, S)
    pl = pull.astype(np.float32).astype(np.int64).reshape(N, 8, 16, M); w = wt.astype(np.int64).reshape(N, 8, 1, 16)[..., :15]
    wl = np.stack([gentries(a) for a in wants]).astype(np.int64).reshape(N, 8, RO, WN); sl = np.stack([gentries(a) for a in snd]).astype(np.int64).reshape(N, 8, N - 1, G)
    gi = np.arange(8)[:, None]; g3 = gi[:, :, None]; lane = np.arange(L)
    req = np.full((N, 8, N - 1, CAP), -1, np.int64)
    for t in range(RO):
        new = x.copy(); ask = np.full((N, 8, N - 1, CAP), -1, np.int64)
        for r in range(N):
            f = np.concatenate([x[r]] + [np.take_along_axis(x[(r - e) % N], sl[(r - e) % N, :, e - 1][:, None, :], 2) for e in range(1, N)], axis=2)
            s = np.concatenate([req[r].reshape(8, -1), wl[r, :, t]], axis=1)
            climb = s >= 0; s = np.maximum(s, 0); climb = climb & (f[gi, 15, s] >= 0); done = np.zeros((8, L), bool)
            for h in range(H):
                c = nbr[r][g3, np.arange(16), np.minimum(s, S - 1)[:, :, None]]
                a = f[g3, :, c]; b = f[gi, :, s][:, :, None, :]
                cov = (a[..., 15] > b[..., 15]) & np.any(a[..., :15] > b[..., :15], axis=3) & np.any(a[..., :15] < b[..., :15], axis=3)
                may = climb & (s < S); cov = cov & may[:, :, None]
                best = np.argmax(np.where(cov, a[..., 15], -1), axis=2)
                hit = np.any(cov, axis=2); done = done | (may & ~hit); climb = climb & hit
                s = np.where(hit, np.take_along_axis(c, best[:, :, None], 2)[:, :, 0], s)
            for e in range(1, N):
                q = (r - e) % N; k = s - S - (e - 1) * G; on = ((k >= 0) & (k < G)).astype(np.int64)
                before = np.add.accumulate(on, axis=1) - on; gs, ls = np.nonzero((on == 1) & (before < CAP))
                ask[q, gs, e - 1, before[gs, ls]] = sl[q, gs, e - 1, k[gs, ls]]
            v = f[gi, :, s]
            z = np.sum(v[:, :, :15] * w[r], axis=2) & (Q - 1); d = ((z * z >> 5) + 97 * t) & (Q - 1); d = np.where(d >= S, d - S, d)
            ok = done & (f[gi, 15, d] < 0); gs, ls = np.nonzero(ok)
            first = np.full((8, S), L, np.int64); np.minimum.at(first, (gs, d[gs, ls]), ls)
            gs, ls = np.nonzero(ok & (first[gi, d] == lane)); dd = d[gs, ls]
            new[r][gs, :15, dd] = (v[gs, ls, :15] + pl[r][gs, :15, dd & (M - 1)]) >> 1
            new[r][gs, 15, dd] = T0 + t; new[r][gs, 15, s[gs, ls]] = -1
        x = new; req = ask
    return {"y": x.reshape(N, 128, S).astype(np.float32).astype(BF)}

@@ -1,0 +1,654 @@
+from concourse.bass import DstId, RemoteDMATransfer
+from concourse.mybir import dt, AluOpType, AxisListType, ActivationFunctionType
+
+ADD, SUB, MUL, MAX, MIN = AluOpType.add, AluOpType.subtract, AluOpType.mult, AluOpType.max, AluOpType.min
+GE, GT, LE, LT, EQ = AluOpType.is_ge, AluOpType.is_gt, AluOpType.is_le, AluOpType.is_lt, AluOpType.is_equal
+SHR, AND = AluOpType.arith_shift_right, AluOpType.bitwise_and
+IDEN, COPY = ActivationFunctionType.Identity, ActivationFunctionType.Copy
+
+N, S, G, CAP, WN, M, RO, H, T0 = 8, 3328, 112, 16, 144, 512, 3, 4, 192
+OWN = 512
+NULL = S + (N - 1) * G
+FW = OWN + NULL + 16
+BW = 120
+K17 = 17 * 8192
+OFS = 99 * K17
+NV = 16
+MAGIC = 12582912.0
+K1 = 4
+
+SCRATCH = {}
+for _n, _w, _t in (
+        ("f", FW, "bfloat16"), ("nbw", NULL + 16, "int32"), ("pl", M, "bfloat16"), ("wti", 1, "int32"), ("wni", 27, "int32"), ("sdi", 49, "int32"),
+        ("sdp", 56, "uint16"), ("sdf", 56, "float32"), ("sdw", 800, "float32"), ("sdx", 784, "float32"), ("wl", 30, "uint16"), ("rep", 50, "uint16"),
+        ("wq", 432, "float32"), ("jf", 128, "float32"), ("jmf", 256, "float32"), ("j4", 128, "float32"), ("j7", 128, "float32"), ("j3", 64, "float32"),
+        ("ji", 64, "int32"), ("cols", 40, "float32"), ("idf", 128, "float32"), ("idh", 128, "float16"), ("idb", 128, "bfloat16"),
+        ("mask", 256, "float32"), ("rep8", 8, "uint16"), ("rep87", 16, "uint16"), ("blk", 128, "float32"), ("wm", 24, "bfloat16"),
+        ("wa", 24, "bfloat16"), ("wb", 264, "bfloat16"), ("wz", 8, "bfloat16"), ("ws", 8, "bfloat16"), ("rsm", 128, "float32"), ("rsa", 112, "float32"),
+        ("rs8", 128, "float32"), ("tril", 128, "bfloat16"), ("ones", 128, "bfloat16"), ("ec", 128, "float32"), ("onf", 128, "float32"),
+        ("gm", 64, "float32"), ("b", 256, "bfloat16"), ("xx", 256, "float32"), ("dx", 256, "float32"), ("dl", 16, "uint16"), ("dlm", 16, "uint16"),
+        ("fd", 256, "bfloat16"), ("uu", 256, "bfloat16"), ("uv", 256, "float32"), ("val", 512, "bfloat16"), ("ex", 256, "float16"), ("da", 256, "float16"),
+        ("trash", 256, "bfloat16"), ("ofl", 32, "uint16"), ("on", 128, "bfloat16"), ("qb", 128, "float32"), ("qs", 128, "float32"),
+        ("mh", 256, "bfloat16"), ("ek", 128, "bfloat16"), ("rq", 64, "float32"), ("gg", 7 * BW, "bfloat16"), ("ld0", 7 * BW, "bfloat16"),
+        ("ld1", 7 * BW, "bfloat16"), ("ld2", 7 * BW, "bfloat16"), ("rki", 8, "uint16"), ("qa", 128, "float32"), ("qc", 128, "float32")):
+    SCRATCH[_n] = ("sbuf", [128, _w], _t)
+for _x in "AB":
+    for _n, _w, _t in (("l", 8, "uint16"), ("off", 128, "uint16"), ("a", 2048, "bfloat16"), ("m", 2048, "bfloat16"), ("cp", 128, "float32"),
+                       ("t1", 128, "float32"), ("u", 128, "float32"), ("k", 128, "float32"), ("sc", 128, "float32")):
+        SCRATCH[_n + _x] = ("sbuf", [128, _w], _t)
+for _n, _t in (("jm3", "float32"), ("dg", "bfloat16"), ("dgs", "float32"), ("trw", "float32"), ("tru", "float32")):
+    SCRATCH[_n] = ("sbuf", [128, 16, 16], _t)
+SCRATCH["e3"] = ("sbuf", [128, 16, 272], "bfloat16")
+for _n in ("accA", "accB", "bpA", "bpB", "q1", "q2", "q3"):
+    SCRATCH[_n] = ("psum", [128, 512], "float32")
+SCRATCH["tri3"] = ("psum", [128, 16, 16], "float32")
+PSUMS = [k for k in SCRATCH if SCRATCH[k][0] == "psum"]
+ALIAS = {}
+for _buf, _t, _names in (
+        ("tf", "float32", (("sL", 16), ("idp", 16), ("alive", 16), ("dT", 16), ("em", 16), ("dmu", 16), ("dc", 16), ("cnt", 16), ("eb", 16), ("kq", 16), ("se", 16),
+                           ("ucode", 16), ("uc2", 16), ("dLc", 16), ("c113", 8), ("rk", 8), ("cm", 8), ("sfA", 8), ("sfB", 8), ("fl", 16), ("base", 32),
+                           ("basm", 32), ("w2", 32), ("of", 32), ("a12", 32), ("wf", 32))),
+        ("ti", "int32", (("vi", 16), ("id0", 16), ("id1", 16), ("zi", 16), ("zm", 16), ("zq", 16), ("zh", 16), ("zg", 16), ("dLi", 16), ("dLm", 16),
+                         ("ebi", 16), ("rpi", 8), ("ci", 8)))):
+    _o = 0
+    for _n, _w in _names:
+        ALIAS[_n] = (_buf, _o, _w)
+        _o += _w
+    SCRATCH[_buf] = ("sbuf", [128, _o], _t)
+SEMAPHORES = ["sv", "ss", "sp", "sg"] + ["d%d" % i for i in range(12)] + ["arr0", "arr1", "arr2"] + ["snd%d" % i for i in range(9)]
+
+
+def R(name, lo=None, hi=None, step=None, rows=128, extra=None):
+    if name in ALIAS:
+        buf, o, w = ALIAS[name]
+        return (buf, o + (0 if lo is None else lo), o + (w if hi is None else hi), step, rows, extra)
+    return (name, lo, hi, step, rows, extra)
+
+
+def rank_program(g, core, T, topo):
+    rank = T.rank_of(core)
+    if rank is None:
+        return
+    qs = {"v": g.vector, "s": g.scalar, "p": g.tensor, "g": g, "y": g.sync}
+    semof = {"v": "sv", "s": "ss", "p": "sp", "g": "sg"}
+    cnt = {"v": 0, "s": 0, "p": 0, "g": 0}
+    known = {"v": {}, "s": {}, "p": {}, "g": {}, "y": {}}
+    hist = {}
+    dman = [0]
+    sent = {}
+
+    def ap(r):
+        name, lo, hi, step, rows, extra = r
+        t = T[name]
+        if extra is not None:
+            return t[(slice(0, rows),) + extra]
+        if lo is None:
+            return t[:] if rows == 128 else t[0:rows]
+        return t[0:rows, lo:hi] if step is None else t[0:rows, lo:hi:step]
+
+    def span(r):
+        name, lo, hi, step, rows, extra = r
+        if extra is not None and not isinstance(extra[0], slice):
+            return name, 1000 * extra[0], 1000 * extra[0] + 1000
+        if name in PSUMS or lo is None:
+            return name, 0, 1 << 20
+        return name, lo, hi
+
+    def emit(q, fn, reads, writes, sem=None, inc=1, dma=False):
+        acc = [(span(r), False) for r in reads] + [(span(r), True) for r in writes]
+        deps = []
+        for (name, lo, hi), w in acc:
+            for rec in hist.get(name, ()):
+                if rec[1] <= lo or rec[0] >= hi:
+                    continue
+                same = rec[3] == q and not dma and not rec[7]
+                if same and name in PSUMS and q == "p":
+                    need = False
+                elif name in PSUMS and not same:
+                    need = True
+                else:
+                    need = rec[2] or w
+                if need:
+                    deps.append(rec)
+        deps.sort(key=lambda rec: -len(rec[6]) * 100000 - rec[5])
+        kn = known[q]
+        for rec in deps:
+            if kn.get(rec[4], 0) >= rec[5]:
+                continue
+            val = rec[5]
+            for o in deps:
+                if o[4] == rec[4]:
+                    val = max(val, o[5])
+            qs[q].wait_ge(T.sem[rec[4]], val)
+            kn[rec[4]] = val
+            for o in deps:
+                if o[4] == rec[4] and o[5] <= val:
+                    for k, v in o[6].items():
+                        if kn.get(k, 0) < v:
+                            kn[k] = v
+        ins = fn()
+        if sem is None:
+            sem = semof[q]
+            cnt[q] += 1
+            val = cnt[q]
+            ins.then_inc(T.sem[sem], 1)
+        else:
+            val = inc
+        snap = dict(kn)
+        snap[sem] = val
+        for (name, lo, hi), w in acc:
+            lst = hist.get(name, [])
+            if w:
+                lst = [rec for rec in lst if not (rec[0] >= lo and rec[1] <= hi)]
+            else:
+                lst = [rec for rec in lst if not (not rec[2] and rec[3] == q and rec[4] == sem and rec[0] >= lo and rec[1] <= hi)]
+            lst.append((lo, hi, w, q, sem, val, snap, dma))
+            hist[name] = lst
+        return ins
+
+    def dma(q, out, in_, outr, inr):
+        sem = "d%d" % dman[0]
+        dman[0] += 1
+        emit(q, lambda: qs[q].dma_start(out, in_).then_inc(T.sem[sem], 16), inr, outr, sem=sem, inc=16, dma=True)
+
+    def ts(out, in0, s1, s2, o0, o1=None, ind=None):
+        rd = [in0] + [x for x in (s1, s2, ind) if isinstance(x, tuple)]
+        a1 = ap(s1) if isinstance(s1, tuple) else s1
+        a2 = ap(s2) if isinstance(s2, tuple) else s2
+        i0 = ap(in0).indirect(ap(ind)) if ind else ap(in0)
+        if o1 is None:
+            emit("v", lambda: g.vector.tensor_scalar(ap(out), i0, a1, None, o0), rd, [out])
+        else:
+            emit("v", lambda: g.vector.tensor_scalar(ap(out), i0, a1, a2, o0, o1), rd, [out])
+
+    def tt(out, in0, in1, op, ind=None):
+        i0 = ap(in0).indirect(ap(ind)) if ind else ap(in0)
+        emit("v", lambda: g.vector.tensor_tensor(ap(out), i0, ap(in1), op), [in0, in1] + ([ind] if ind else []), [out])
+
+    def tc(out, in_, ind=None, oind=None):
+        i0 = ap(in_).indirect(ap(ind)) if ind else ap(in_)
+        o = ap(out).indirect(ap(oind)) if oind else ap(out)
+        emit("v", lambda: g.vector.tensor_copy(o, i0), [in_] + ([ind] if ind else []) + ([oind] if oind else []), [out])
+
+    def scan(out, d0, d1, init, o0, o1):
+        emit("v", lambda: g.vector.tensor_tensor_scan(ap(out), ap(d0), ap(d1), init, o0, o1), [d0, d1], [out])
+
+    def ms(out, c):
+        emit("v", lambda: g.vector.memset(ap(out), c), [], [out])
+
+    def act(out, in_, func, bias=None, scale=None, ind=None, accum=None):
+        i0 = ap(in_).indirect(ap(ind)) if ind else ap(in_)
+        kw = {}
+        rd = [in_] + ([ind] if ind else [])
+        wr = [out]
+        if bias is not None:
+            kw["bias"] = ap(bias)
+            rd.append(bias)
+        if scale is not None:
+            kw["scale"] = ap(scale)
+            rd.append(scale)
+        if accum is not None:
+            kw["accum_out"] = ap(accum)
+            wr.append(accum)
+        emit("s", lambda: g.scalar.activation(ap(out), i0, func, **kw), rd, wr)
+
+    def mm(out, lhsT, rhs, start, stop):
+        emit("p", lambda: g.tensor.matmul(ap(out), ap(lhsT), ap(rhs), start, stop), [lhsT, rhs], [out])
+
+    def iota(out, pattern, base, cmul, flt=True):
+        if flt:
+            emit("g", lambda: g.iota(ap(out), pattern, base, cmul, allow_small_or_imprecise_dtypes=True), [], [out])
+        else:
+            emit("g", lambda: g.iota(ap(out), pattern, base, cmul), [], [out])
+
+    COL = {}
+
+    def col(name):
+        if name not in COL:
+            COL[name] = len(COL)
+        return R("cols", COL[name], COL[name] + 1)
+
+    hx = S // 2
+    dma("y", T.sdi[:], T.snd[:], [R("sdi")], [])
+    dma("s", T.f[:, OWN + hx:OWN + S], T.x0[:, hx:S], [R("f", OWN + hx, OWN + S)], [])
+    dma("y", T.f[:, OWN:OWN + hx], T.x0[:, 0:hx], [R("f", OWN, OWN + hx)], [])
+    dma("s", T.wti[:], T.wt[:], [R("wti")], [])
+    dma("y", T.wni[:], T.wants[:], [R("wni")], [])
+    dma("s", T.nbw[:, hx:S], T.nb[:, hx:S], [R("nbw", hx, S)], [])
+    dma("y", T.nbw[:, 0:hx], T.nb[:, 0:hx], [R("nbw", 0, hx)], [])
+    dma("y", T.pl[:], T.pull[:], [R("pl")], [])
+
+    iota(R("ci", 0, 1), [[0, 1]], 0, 1, False)
+    iota(R("jf"), [[1, 128]], 0, 0)
+    iota(R("jmf"), [[0, 16], [1, 16]], 0, 0)
+    iota(R("j4"), [[1, 8], [0, 16]], 0, 0)
+    iota(R("ji"), [[1, 64]], 0, 0, False)
+    iota(R("nbw", S, NULL + 1), [[1, NULL + 1 - S]], S, 0, False)
+
+    ms(R("gg"), 0.0)
+    for nm in ("id0", "id1"):
+        ms(R(nm), 0)
+    ms(R("alive"), 0.0)
+    ms(R("cnt"), 0.0)
+    ms(R("q1", 0, 64), 0.0)
+    ms(R("q3", 0, 128), 0.0)
+    ms(R("f", OWN + NULL, FW), -1.0)
+    ms(R("ones"), 1.0)
+    ms(R("wm", 0, 8), 0.0)
+    ms(R("wa", 16, 24), 0.0)
+    ts(R("ci", 1, 2), R("ci", 0, 1), 15, None, AND)
+    ts(R("ci", 2, 3), R("ci", 0, 1), 4, None, SHR)
+    tc(col("p"), R("ci", 0, 1))
+    tc(col("q"), R("ci", 1, 2))
+    tc(col("g"), R("ci", 2, 3))
+    ts(R("ci", 3, 4), R("ci", 1, 2), 3, None, SHR)
+    for e in range(7):
+        tc(R("sdp", 8 * e, 8 * e + 7), R("sdi", 7 * e, 7 * e + 7))
+    P34, P26 = float(2 ** 34), float(2 ** 26)
+    ts(col("r15"), col("q"), 15.0, None, EQ)
+    ts(col("rl"), col("q"), 15.0, None, LT)
+    ts(col("b2"), col("r15"), 2.0, None, MUL)
+    ts(col("nb"), col("q"), -8192.0, -8192.0 - OFS, MUL, ADD)
+    ts(col("k17"), col("r15"), float(K17), None, MUL)
+    ts(col("t34"), col("rl"), P34, None, MUL)
+    ts(col("m34"), col("rl"), -P34, None, MUL)
+    ts(col("m26"), col("r15"), -P26, None, MUL)
+    tt(col("mt2"), col("m34"), col("m26"), ADD)
+    ts(R("cm"), R("jf", 0, 8), col("g"), None, EQ)
+    ts(R("idf"), R("jf"), col("p"), None, EQ)
+    ts(R("blk"), R("j4"), col("g"), None, EQ)
+    act(R("idb"), R("idf"), COPY)
+    for k in (1, 2):
+        act(R("wm", 8 * k, 8 * k + 8), R("cm"), COPY, scale=col("t34"))
+    act(R("wa", 0, 8), R("cm"), COPY, scale=col("k17"))
+    act(R("wa", 8, 16), R("cm"), COPY, scale=col("m34"))
+    act(R("wb", 0, 128), R("blk"), COPY, scale=col("m26"))
+    act(R("wb", 128, 256), R("blk"), COPY, scale=col("mt2"))
+    act(R("wb", 256, 264), R("cm"), COPY, scale=col("k17"))
+    act(R("ws"), R("cm"), COPY, scale=col("r15"))
+    ts(R("mask"), R("jmf"), col("q"), None, EQ)
+    ts(R("rsm"), R("jmf", 0, 128), 0.0, -1e29, EQ, MUL)
+
+    off = [e for e in range(1, 8) if topo.chip(T.cores[(rank + e) % N]) != topo.chip(core)]
+    near = [e for e in range(1, 8) if e not in off]
+    calls = [off[0:4], off[4:] + near]
+
+    def ghosts(t):
+        order = calls[0] + calls[1]
+        for e in order:
+            o, w, i = R("gg", (e - 1) * BW, (e - 1) * BW + G), R("f", OWN, OWN + S), R("sdp", 8 * (e - 1), 8 * e - 1)
+            if e == order[-1] or (t == 0 and e in order[-3:]):
+                tc(o, w, ind=i)
+            else:
+                act(o, w, COPY, ind=i)
+
+    def engines_of(src, es, e):
+        me = T.cores[src]
+        away = [x for x in es if topo.chip(T.cores[(src + x) % N]) != topo.chip(me)]
+        out = {}
+        used = []
+        for x in away + [y for y in es if y not in away]:
+            eng = topo.engines(me, T.cores[(src + x) % N])
+            free = [y for y in eng if y not in used]
+            room = len(eng) // len(away) if x in away else len(free)
+            n = 1
+            while n * 2 <= room:
+                n *= 2
+            out[x] = free[0:n]
+            used = used + out[x]
+        return out[e]
+
+    def send(t):
+        for k, es in enumerate(calls):
+            trs = []
+            inc = 0
+            for e in es:
+                dst = T.cores[(rank + e) % N]
+                mine = engines_of(rank, es, e)
+                rid, pid, se = topo.addr(dst)
+                mk = 0
+                for x in mine:
+                    mk += 1 << x
+                p = 7 - e
+                trs.append(RemoteDMATransfer(dst_ids=[DstId(rid=rid, pnc=pid)], dma_engine_mask=mk, remote_sem=T.sem["arr%d" % t],
+                                             srcs=[T.gg[:, (e - 1) * BW:e * BW]], dsts=[T["ld%d" % t][:, p * BW:(p + 1) * BW]]))
+                inc += len(mine)
+            sem = "snd%d" % (3 * t + k)
+            emit("g", lambda: g.remote_dma_fused(trs, local_sem=T.sem[sem]), [R("gg", (e - 1) * BW, e * BW) for e in es], [], sem=sem, inc=inc, dma=True)
+            sent[sem] = inc
+        arrived = 0
+        for e in range(1, 8):
+            src = (rank - e) % N
+            soff = [x for x in range(1, 8) if topo.chip(T.cores[(src + x) % N]) != topo.chip(T.cores[src])]
+            snear = [x for x in range(1, 8) if x not in soff]
+            arrived += len(engines_of(src, soff[0:4] if e in soff[0:4] else soff[4:] + snear, e))
+        hist["ld%d" % t] = [(0, 1 << 20, True, "r", "arr%d" % t, arrived, {}, True)]
+
+    ghosts(0)
+    send(0)
+    iota(R("j7"), [[0, 16], [1, 8]], 0, 0)
+    iota(R("j3"), [[1, 8], [0, 8]], 0, 0)
+    iota(R("jm3"), [[0, 16], [1, 16]], 0, 0)
+    iota(R("c113"), [[113, 8]], 0, 0)
+
+    tc(R("rep"), R("ji", 0, 50))
+    tc(R("wl", 0, 9), R("wni", 0, 9))
+    ms(R("wf"), 0.0)
+    tc(R("wf", 0, 27), R("wni"))
+    tt(R("wq", 0, 144), R("wf", 0, 32), R("mask", 0, 144), MUL, ind=R("rep", 0, 9))
+
+    def setup_hops():
+        tc(col("wt"), R("wti"))
+        tt(col("wtl"), col("wt"), col("rl"), MUL)
+        act(R("wz"), R("cm"), COPY, scale=col("wtl"))
+        ts(col("neg"), col("r15"), -1.0, None, MUL)
+        ts(col("half"), col("rl"), 0.5, None, MUL)
+        ts(col("q0"), col("rl"), -0.25, None, MUL)
+        for t in range(RO):
+            ts(col("st%d" % t), col("r15"), float(T0 + t), None, MUL)
+            tt(col("nb%d" % t), col("st%d" % t), col("q0"), ADD)
+        for t in (1, 2):
+            tc(R("wl", 10 * t + 1, 10 * t + 10), R("wni", 9 * t, 9 * t + 9))
+        tc(R("idh"), R("idf"))
+        ts(R("rs8"), R("j7"), 0.0, None, GT)
+        ts(R("ec"), R("j7"), -1.0, 7.0, MUL, ADD)
+        ts(R("onf"), R("j7"), 7.0, 99.0, EQ, MUL)
+        tt(R("ec"), R("ec"), R("onf"), ADD)
+        ts(R("tril"), R("jf"), col("p"), None, GT)
+        ts(R("gm"), R("j3"), col("g"), None, EQ)
+        ts(R("trw"), R("jm3"), col("q"), 1.5, LT, MUL)
+        ts(R("tru"), R("jm3"), col("q"), -0.5, LE, MUL)
+        tt(R("tri3"), R("trw"), R("tru"), ADD)
+        ts(R("base"), R("jf", 0, 32), 16.0, col("q"), MUL, ADD)
+        ts(R("basm"), R("base"), float(-OWN), None, ADD)
+        for h in (0, 1):
+            ts(R("ucode", 8 * h, 8 * h + 8), R("jf", 0, 8), 0.0, float(S - 2048 + 128 * h), MUL, ADD)
+        ts(R("ucode"), R("ucode"), col("p"), None, ADD)
+        ts(R("uc2"), R("ucode"), 2048.0, None, ADD)
+        tc(col("q8"), R("ci", 3, 4))
+        ts(R("rk"), R("jf", 0, 8), 2.0, col("q8"), MUL, ADD)
+        tc(R("rep8"), R("rk"))
+        ts(R("zi"), R("ji", 0, 16), 8.0, 7.0, MUL, ADD)
+        tc(R("rep87"), R("zi"))
+
+    def setup_later():
+        for t in (1, 2):
+            w0 = 8 * ((9 * t) // 8)
+            for lo, n in ((0, 8), (8, 1)):
+                ts(R("rpi", 0, n), R("ji", 0, n), float(9 * t - w0 + lo), None, ADD)
+                tc(R("rki", 0, n), R("rpi", 0, n))
+                tt(R("wq", 144 * t + 16 * lo, 144 * t + 16 * lo + 16 * n), R("wf", w0, 32), R("mask", 0, 16 * n), MUL, ind=R("rki", 0, n))
+        tc(R("sdf", 0, 49), R("sdi"))
+        ms(R("sdf", 49, 56), 0.0)
+        for lo in range(0, 49, 16):
+            hi = min(49, lo + 16)
+            tt(R("sdx", 16 * lo, 16 * hi), R("sdf"), R("mask", 0, 16 * (hi - lo)), MUL, ind=R("rep", lo, hi))
+        ms(R("sdw", 0, 784, 113), float(NULL))
+        ts(R("rsa"), R("jmf", 0, 112), 0.0, None, GT)
+        for lo, hi in ((0, 4 * G), (4 * G, 7 * G)):
+            mm(R("q2", 0, hi - lo), R("blk"), R("sdx", lo, hi), True, True)
+            for e in range(lo // G, hi // G):
+                act(R("sdw", 113 * e + 1, 113 * e + 113), R("q2", e * G - lo, (e + 1) * G - lo), COPY)
+
+    def stream(X, t):
+        h = 0 if X == "A" else 1
+        nc = (4, 5)[h] if t == 0 else 8
+        c0 = 0 if h == 0 else (4 if t == 0 else 8)
+        return {"X": X, "h": h, "nl": 16 * nc, "nc": nc, "c0": c0, "l0": 16 * c0, "hop": 1, "t": t}
+
+    def start(st):
+        X, t, h, nl = st["X"], st["t"], st["h"], st["nl"]
+        if t == 0:
+            st["list"] = R("wl", st["c0"], st["c0"] + st["nc"])
+            src = R("wq", st["l0"], st["l0"] + nl)
+        elif h == 1:
+            st["list"] = R("wl", 10 * t + 2, 10 * t + 10)
+            src = R("wq", 144 * t + 16, 144 * t + 144)
+        else:
+            tt(R("rk", 0, 7), R("ld%d" % t, G, 7 * BW, BW), R("c113", 0, 7), ADD)
+            tc(R("rki", 0, 7), R("rk", 0, 7))
+            tt(R("qa", 0, 112), R("sdw", 0, 791), R("mask", 0, 112), MUL, ind=R("rki", 0, 7))
+            tc(R("lA", 7, 8), R("wl", 10 * t + 1, 10 * t + 2))
+            scan(R("qc", 0, 112), R("rsa"), R("qa", 0, 112), 0.0, MUL, ADD)
+            tc(R("lA", 0, 7), R("qc", 15, 112, 16))
+            act(R("qa", 112, 128), R("wq", 144 * t, 144 * t + 16), COPY)
+            st["list"] = R("lA")
+            src = R("qa")
+        mm(R("bp" + X, 136, 144, rows=nl), src, R("cm"), True, True)
+        nbg(st)
+        ts(R("idp", 8 * h, 8 * h + 8, rows=nl), R("bp" + X, 136, 144, rows=nl), float(-OFS), None, ADD)
+
+    def nbg(st):
+        X, nl = st["X"], st["nl"]
+        tc(R("off" + X, 0, nl), R("nbw"), ind=st["list"])
+
+    def compv(st):
+        X, nl = st["X"], st["nl"]
+        ts(R("cp" + X, 0, nl), R("off" + X, 0, nl), col("nb"), None, ADD)
+
+    def bgat(st):
+        X, h, nl, l0 = st["X"], st["h"], st["nl"], st["l0"]
+        bb = R("b", l0, l0 + nl)
+        ts(bb, R("f", OWN, FW), col("b2"), None, ADD, ind=st["list"])
+        mm(R("bp" + X, 0, nl), R("idb"), bb, True, True)
+        mm(R("acc" + X, 128, 392, rows=nl), bb, R("wb"), True, False)
+        mm(R("acc" + X, 0, 128, rows=nl), R("cp" + X, 0, nl), R("idf"), False, False)
+        if st["hop"] == H:
+            mm(R("q1", 8 * h, 8 * h + 8, rows=nl), bb, R("wz"), True, True)
+
+    def chunk(st, k):
+        n2 = 64 if st["nl"] == 128 else st["nl"]
+        return (0, n2) if k == 0 else (n2, st["nl"])
+
+    def agat(st, k):
+        X = st["X"]
+        lo, hi = chunk(st, k)
+        if hi > lo:
+            act(R("a" + X, 16 * lo, 16 * hi), R("f", OWN, FW), IDEN, bias=col("b2"), ind=R("off" + X, lo, hi))
+
+    def amm(st):
+        X, nl = st["X"], st["nl"]
+        for n in range(NV):
+            mm(R("acc" + X, n, 384, 16, rows=nl), R("a" + X, n, 16 * nl, 16), R("wa"), False, False)
+
+    def maxes(st, k, ns):
+        X, nl = st["X"], st["nl"]
+        lo, hi = chunk(st, k)
+        for n in ns:
+            if hi > lo:
+                tt(R("m" + X, n * nl + lo, n * nl + hi), R("a" + X, 16 * lo + n, 16 * hi, 16), R("bp" + X, lo, hi), MAX)
+            if k == 1:
+                mm(R("acc" + X, n, 384, 16, rows=nl), R("m" + X, n * nl, (n + 1) * nl), R("wm"), False, n == NV - 1)
+
+    def tail(st):
+        X, h, nl, hop = st["X"], st["h"], st["nl"], st["hop"]
+        acc = "acc" + X
+        hh = (8 * h, 8 * h + 8)
+        act(R("t1" + X, rows=nl), R(acc, 128, 256, rows=nl), COPY)
+        tt(R("u" + X, rows=nl), R("t1" + X, rows=nl), R(acc, 256, 384, rows=nl), MIN)
+        tt(R("k" + X, rows=nl), R("u" + X, rows=nl), R(acc, 0, 128, rows=nl), MIN)
+        tt(R("sf" + X, rows=nl), R("idp", hh[0], hh[1], rows=nl), R(acc, 384, 392, rows=nl), ADD)
+        scan(R("sc" + X, rows=nl), R("rsm", rows=nl), R("k" + X, rows=nl), -1e29, ADD, MAX)
+        if hop == 1:
+            ts(R("alive", hh[0], hh[1], rows=nl), R(acc, 384, 392, rows=nl), 1.5 * K17, None, GE)
+        tt(R("vi", hh[0], hh[1], rows=nl), R("sc" + X, 15, 128, 16, rows=nl), R("sf" + X, rows=nl), MAX)
+        ts(R("id%d" % (hop % 2), hh[0], hh[1], rows=nl), R("vi", hh[0], hh[1], rows=nl), 8191, None, AND)
+        if hop < H:
+            tt(R("xx", 128 * h, 128 * h + 128), R("id%d" % (hop % 2), hh[0], hh[1]), R("mask", 0, 128), MUL, ind=R("rep", 0, 8))
+            mm(R("bp" + X, 128, 128 + st["nc"]), R("xx", 128 * h, 128 * h + 128, rows=nl), R("cm", 0, st["nc"], rows=nl), True, True)
+
+    def nextlist(st):
+        X, h, nl, hop, nc = st["X"], st["h"], st["nl"], st["hop"], st["nc"]
+        tc(R("l" + X, 0, nc), R("bp" + X, 128, 128 + nc))
+        st["list"] = R("l" + X, 0, nc)
+        nbg(st)
+        ts(R("idp", 8 * h, 8 * h + 8, rows=nl), R("id%d" % (hop % 2), 8 * h, 8 * h + 8, rows=nl), float(-OFS), None, ADD)
+        if hop == H - 1:
+            tc(R("sL", st["c0"], st["c0"] + nc), R("bp" + X, 128, 128 + nc))
+        st["hop"] = hop + 1
+
+    def places(t, sts):
+        tc(R("zi"), R("q1", 0, 16))
+        ts(R("zm"), R("zi"), 4095, None, AND)
+        tt(R("zq"), R("zm"), R("zm"), MUL)
+        if t:
+            ts(R("zi"), R("zq"), float(97 * 32 * t), None, ADD)
+        ts(R("zh"), R("zi" if t else "zq"), 5, 4095, SHR, AND)
+        ts(R("zg"), R("zh"), float(S), float(-S), GE, MUL)
+        tt(R("dT"), R("zh"), R("zg"), ADD)
+        tt(R("dx"), R("dT"), R("mask", 0, 256), MUL, ind=R("rep", 0, 16))
+        for st in sts:
+            mm(R("q1", 16 + st["c0"], 16 + st["c0"] + st["nc"]), R("dx", 128 * st["h"], 128 * st["h"] + 128, rows=st["nl"]),
+               R("cm", 0, st["nc"], rows=st["nl"]), True, True)
+
+    def places2(t, sts):
+        nc = sum(st["nc"] for st in sts)
+        L = 16 * nc
+        tc(R("dLi", 0, nc), R("q1", 16, 16 + nc))
+        tc(R("dl", 0, nc), R("dLi", 0, nc))
+        act(R("fd", 0, L), R("f", OWN, OWN + S), COPY, ind=R("dl", 0, nc))
+        ts(R("dLm", 0, nc), R("dLi", 0, nc), M - 1, None, AND)
+        tc(R("dlm", 0, nc), R("dLm", 0, nc))
+        act(R("uu", 0, L), R("pl"), COPY, ind=R("dlm", 0, nc))
+        ts(R("dLc", 0, nc), R("dLi", 0, nc), -2048.0, None, ADD)
+        tt(R("dmu"), R("dT"), R("uc2"), SUB)
+        ts(R("se"), R("id1"), float(S), None, LT)
+        tt(R("se"), R("se"), R("alive"), MUL)
+        tt(R("dmu"), R("dmu"), R("se"), MUL)
+        tt(R("a12", 0, nc), R("dLi", 0, nc), R("basm", 0, nc), SUB)
+        tt(R("a12", nc, 2 * nc), R("sL", 0, nc), R("basm", nc, 2 * nc), SUB)
+
+    def places3(t, sts):
+        nc = sum(st["nc"] for st in sts)
+        L = 16 * nc
+        for st in sts:
+            mm(R("q1", 32 + 8 * st["h"], 40 + 8 * st["h"], rows=st["nl"]), R("fd", st["l0"], st["l0"] + st["nl"]), R("ws"), True, True)
+        mm(R("q2", 0, L), R("idb"), R("uu", 0, L), True, False)
+        mm(R("q2", 0, L), R("idb"), R("b", 0, L), False, True)
+        ts(R("em"), R("q1", 32, 48), 0.0, None, LT)
+        tt(R("dmu"), R("em"), R("dmu"), MUL)
+
+    def moves(t, sts):
+        nc = sum(st["nc"] for st in sts)
+        L = 16 * nc
+        act(R("uv", 0, L), R("q2", 0, L), IDEN, bias=col("nb%d" % t), scale=col("half"))
+        act(R("val", L, 2 * L), R("b", 0, L), IDEN, bias=col("neg"), scale=col("rl"))
+        tt(R("se"), R("id0"), R("id1"), EQ)
+        tt(R("dc"), R("se"), R("dmu"), MUL)
+        tt(R("dc"), R("dc"), R("ucode"), ADD)
+        tc(R("ex"), R("dc"), ind=R("rep", 0, 16))
+        for st in sts:
+            mm(R("q2", st["l0"], st["l0"] + st["nl"]), R("ex", 128 * st["h"], 128 * st["h"] + 128, rows=st["nl"]), R("idh", 0, st["nl"], rows=st["nl"]), True, True)
+        ts(R("val", 0, L), R("uv", 0, L), MAGIC, -MAGIC, ADD, ADD)
+        tc(R("da", 0, L), R("q2", 0, L))
+        for c in range(nc - 1, -1, -1):
+            ts(R("e3", extra=(c, slice(256 - 16 * c, 272))), R("da", 0, 16 * c + 16), R("dLc", c, c + 1), None, EQ)
+            if c:
+                act(R("trash", 0, 16 * c), R("e3", extra=(c, slice(256 - 16 * c, 256))), COPY, accum=R("cnt", c, c + 1))
+        sl = slice(0, nc)
+        tt(R("dg", extra=(sl, slice(0, 16))), R("e3", extra=(sl, slice(256, 272))), R("tri3", extra=(sl, slice(0, 16))), MUL)
+        for w in (8, 4, 2, 1):
+            src = "dg" if w == 8 else "dgs"
+            tt(R("dgs", extra=(sl, slice(0, w))), R(src, extra=(sl, slice(0, w))), R(src, extra=(sl, slice(w, 2 * w))), ADD)
+
+    def moves2(t, sts):
+        nc = sum(st["nc"] for st in sts)
+        L = 16 * nc
+        tt(R("fl", 0, nc), R("cnt", 0, nc), R("dgs", extra=(slice(0, nc), 0)), ADD)
+        for k in (0, nc):
+            ts(R("w2", k, k + nc), R("fl", 0, nc), -0.25, None, LT)
+        tt(R("of", 0, 2 * nc), R("w2", 0, 2 * nc), R("a12", 0, 2 * nc), MUL)
+        tt(R("of", 0, 2 * nc), R("of", 0, 2 * nc), R("base", 0, 2 * nc), ADD)
+        tc(R("ofl", 0, 2 * nc), R("of", 0, 2 * nc))
+        tc(R("f", 0, OWN + S), R("val", 0, 2 * L), oind=R("ofl", 0, 2 * nc))
+
+    def requests(sts, part):
+        if part == 0:
+            ts(R("ebi"), R("id0"), 1.0 / G, 1.0 - (S + (G - 1) / 2) / G, MUL, ADD)
+            tt(R("eb"), R("ebi"), R("alive"), MUL)
+            ts(R("kq"), R("ebi"), float(-G), float(-(S - G - 1)), MUL, ADD)
+            tt(R("kq"), R("kq"), R("id0"), ADD)
+            tt(R("on"), R("eb"), R("ec"), EQ, ind=R("rep8"))
+            for st in sts:
+                nl, h = st["nl"], st["h"]
+                if h == 0:
+                    mm(R("q3", 0, 64, rows=nl), R("tril", 0, nl, rows=nl), R("on", 0, 64, rows=nl), True, True)
+                else:
+                    n0 = sts[0]["nl"]
+                    mm(R("q3", 64, 128, rows=nl), R("tril", 0, nl, rows=nl), R("on", 64, 128, rows=nl), True, False)
+                    mm(R("q3", 64, 128, rows=nl), R("ones", 0, nl, rows=n0), R("on", 0, 64, rows=n0), False, True)
+        elif part == 1:
+            tt(R("qb"), R("on"), R("q3", 0, 128), MUL)
+            scan(R("qs"), R("rs8"), R("qb"), 0.0, MUL, ADD)
+            tt(R("mh"), R("qs"), R("jmf"), EQ, ind=R("rep87"))
+            tt(R("ek"), R("kq"), R("on"), MUL, ind=R("rep8"))
+            for st in sts:
+                nl, h = st["nl"], st["h"]
+                mm(R("q3", 128, 192), R("mh", 128 * h, 128 * h + 128, rows=nl), R("ek", 64 * h, 64 * h + 64, rows=nl), h == 0, h == 1)
+        else:
+            tt(R("rq"), R("gm"), R("q3", 128, 192), MUL)
+            tt(R("rq", 0, 32), R("rq", 0, 32), R("rq", 32, 64), ADD)
+            tt(R("rq", 0, 16), R("rq", 0, 16), R("rq", 16, 32), ADD)
+            tt(R("gg", G, 7 * BW, BW), R("rq", 0, 7), R("rq", 8, 15), ADD)
+
+    def landed(t):
+        for e in range(1, 8):
+            o, i = R("f", OWN + S + (e - 1) * G, OWN + S + e * G), R("ld%d" % t, (7 - e) * BW, (7 - e) * BW + G)
+            if e in (2, 5):
+                act(o, i, COPY)
+            else:
+                tc(o, i)
+
+    for t in range(RO):
+        A, B = stream("A", t), stream("B", t)
+        sts = (A, B)
+        order = (A, B) if t == 0 else (B, A)
+        if t == 1:
+            setup_later()
+        start(order[0])
+        compv(order[0])
+        if t == 0:
+            setup_hops()
+        landed(t)
+        for slot in range(2 * H):
+            X, Y = order[slot % 2], order[1 - slot % 2]
+            last = slot == 2 * H - 1
+            if slot:
+                compv(X)
+            bgat(X)
+            agat(X, 0)
+            if slot == 0:
+                start(Y)
+                maxes(X, 0, range(NV))
+            else:
+                tail(Y)
+                maxes(X, 0, range(0, K1))
+                if last:
+                    places(t, sts)
+                else:
+                    nextlist(Y)
+                maxes(X, 0, range(K1, NV))
+            agat(X, 1)
+            amm(X)
+            if last:
+                places2(t, sts)
+            maxes(X, 1, range(NV))
+        places3(t, sts)
+        tail(order[1])
+        moves(t, sts)
+        if t + 1 < RO:
+            requests(sts, 0)
+        moves2(t, sts)
+        if t + 1 < RO:
+            requests(sts, 1)
+            ghosts(t + 1)
+            requests(sts, 2)
+            send(t + 1)
+    emit("y", lambda: g.sync.dma_start(T.y[:], T.f[:, OWN:OWN + S]).then_inc(T.sem["d11"], 16), [R("f", OWN, OWN + S)], [], sem="d11", inc=16, dma=True)
+    g.sync.wait_ge(T.sem["d11"], 16)
+    for q in ("v", "s", "p", "g"):
+        g.wait_ge(T.sem[semof[q]], cnt[q])
+    for name, val in sorted(sent.items()):
+        g.wait_ge(T.sem[name], val)
+    for i in range(dman[0]):
+        g.wait_ge(T.sem["d%d" % i], 16)

@@ -14,8 +14,10 @@ BW = 120
 K17 = 17 * 8192
 OFS = 99 * K17
 NV = 16
+RR = 4
+NC = NV // RR
 MAGIC = 12582912.0
-K1 = 4
+K1 = 2
 
 SCRATCH = {}
 for _n, _w, _t in (
@@ -25,7 +27,7 @@ for _n, _w, _t in (
         ("ji", 64, "int32"), ("cols", 40, "float32"), ("idf", 128, "float32"), ("idh", 128, "float16"), ("idb", 128, "bfloat16"),
         ("mask", 256, "float32"), ("rep8", 8, "uint16"), ("rep87", 16, "uint16"), ("blk", 128, "float32"), ("wm", 24, "bfloat16"),
         ("wa", 24, "bfloat16"), ("wb", 264, "bfloat16"), ("wz", 8, "bfloat16"), ("ws", 8, "bfloat16"), ("rsm", 128, "float32"), ("rsa", 112, "float32"),
-        ("rs8", 128, "float32"), ("tril", 128, "bfloat16"), ("ones", 128, "bfloat16"), ("ec", 128, "float32"), ("onf", 128, "float32"),
+        ("rs8", 128, "float32"), ("tril", 128, "bfloat16"), ("ones", 128, "bfloat16"), ("k9", 8, "bfloat16"), ("ec", 128, "float32"), ("onf", 128, "float32"),
         ("gm", 64, "float32"), ("b", 256, "bfloat16"), ("xx", 256, "float32"), ("dx", 256, "float32"), ("dl", 16, "uint16"), ("dlm", 16, "uint16"),
         ("fd", 256, "bfloat16"), ("uu", 256, "bfloat16"), ("uv", 256, "float32"), ("val", 512, "bfloat16"), ("ex", 256, "float16"), ("da", 256, "float16"),
         ("trash", 256, "bfloat16"), ("ofl", 32, "uint16"), ("on", 128, "bfloat16"), ("qb", 128, "float32"), ("qs", 128, "float32"),
@@ -234,6 +236,7 @@ def rank_program(g, core, T, topo):
     ms(R("q3", 0, 128), 0.0)
     ms(R("f", OWN + NULL, FW), -1.0)
     ms(R("ones"), 1.0)
+    ms(R("k9"), -11.0 * K17)
     ms(R("wm", 0, 8), 0.0)
     ms(R("wa", 16, 24), 0.0)
     ts(R("ci", 1, 2), R("ci", 0, 1), 15, None, AND)
@@ -414,9 +417,9 @@ def rank_program(g, core, T, topo):
             act(R("qa", 112, 128), R("wq", 144 * t, 144 * t + 16), COPY)
             st["list"] = R("lA")
             src = R("qa")
-        mm(R("bp" + X, 136, 144, rows=nl), src, R("cm"), True, True)
+        mm(R("acc" + X, 408, 416, rows=nl), src, R("cm"), True, True)
         nbg(st)
-        ts(R("idp", 8 * h, 8 * h + 8, rows=nl), R("bp" + X, 136, 144, rows=nl), float(-OFS), None, ADD)
+        tc(R("idp", 8 * h, 8 * h + 8, rows=nl), R("acc" + X, 408, 416, rows=nl))
 
     def nbg(st):
         X, nl = st["X"], st["nl"]
@@ -430,21 +433,22 @@ def rank_program(g, core, T, topo):
         X, h, nl, l0 = st["X"], st["h"], st["nl"], st["l0"]
         bb = R("b", l0, l0 + nl)
         ts(bb, R("f", OWN, FW), col("b2"), None, ADD, ind=st["list"])
-        mm(R("bp" + X, 0, nl), R("idb"), bb, True, True)
+        for j in range(RR):
+            mm(R("bp" + X, j, RR * nl, RR), R("idb"), bb, True, True)
         mm(R("acc" + X, 128, 392, rows=nl), bb, R("wb"), True, False)
+        mm(R("acc" + X, 384, 392, rows=nl), R("ones", 0, nl, rows=9), R("k9", rows=9), False, False)
         mm(R("acc" + X, 0, 128, rows=nl), R("cp" + X, 0, nl), R("idf"), False, False)
         if st["hop"] == H:
             mm(R("q1", 8 * h, 8 * h + 8, rows=nl), bb, R("wz"), True, True)
 
     def chunk(st, k):
-        n2 = 64 if st["nl"] == 128 else st["nl"]
+        n2 = 64 if st["nl"] == 128 else 32
         return (0, n2) if k == 0 else (n2, st["nl"])
 
     def agat(st, k):
         X = st["X"]
         lo, hi = chunk(st, k)
-        if hi > lo:
-            act(R("a" + X, 16 * lo, 16 * hi), R("f", OWN, FW), IDEN, bias=col("b2"), ind=R("off" + X, lo, hi))
+        act(R("a" + X, 16 * lo, 16 * hi), R("f", OWN, FW), IDEN, bias=col("b2"), ind=R("off" + X, lo, hi))
 
     def amm(st):
         X, nl = st["X"], st["nl"]
@@ -455,36 +459,36 @@ def rank_program(g, core, T, topo):
         X, nl = st["X"], st["nl"]
         lo, hi = chunk(st, k)
         for n in ns:
-            if hi > lo:
-                tt(R("m" + X, n * nl + lo, n * nl + hi), R("a" + X, 16 * lo + n, 16 * hi, 16), R("bp" + X, lo, hi), MAX)
+            tt(R("m" + X, RR * (n * nl + lo), RR * (n * nl + hi)), R("a" + X, 16 * lo + n, 16 * hi, NC), R("bp" + X, RR * lo, RR * hi), MAX)
             if k == 1:
-                mm(R("acc" + X, n, 384, 16, rows=nl), R("m" + X, n * nl, (n + 1) * nl), R("wm"), False, n == NV - 1)
+                for j in range(RR):
+                    mm(R("acc" + X, n + NC * j, 384, 16, rows=nl), R("m" + X, RR * n * nl + j, RR * (n + 1) * nl, RR), R("wm"), False,
+                       n == NC - 1 and j == RR - 1)
 
     def tail(st):
         X, h, nl, hop = st["X"], st["h"], st["nl"], st["hop"]
         acc = "acc" + X
         hh = (8 * h, 8 * h + 8)
-        act(R("t1" + X, rows=nl), R(acc, 128, 256, rows=nl), COPY)
+        tc(R("t1" + X, rows=nl), R(acc, 128, 256, rows=nl))
         tt(R("u" + X, rows=nl), R("t1" + X, rows=nl), R(acc, 256, 384, rows=nl), MIN)
         tt(R("k" + X, rows=nl), R("u" + X, rows=nl), R(acc, 0, 128, rows=nl), MIN)
-        tt(R("sf" + X, rows=nl), R("idp", hh[0], hh[1], rows=nl), R(acc, 384, 392, rows=nl), ADD)
+        tt(R("sf" + X, rows=nl), R("idp" if hop == 1 else "id%d" % (1 - hop % 2), hh[0], hh[1], rows=nl), R(acc, 384, 392, rows=nl), ADD)
         scan(R("sc" + X, rows=nl), R("rsm", rows=nl), R("k" + X, rows=nl), -1e29, ADD, MAX)
         if hop == 1:
-            ts(R("alive", hh[0], hh[1], rows=nl), R(acc, 384, 392, rows=nl), 1.5 * K17, None, GE)
+            ts(R("alive", hh[0], hh[1], rows=nl), R(acc, 384, 392, rows=nl), 1.5 * K17 - OFS, None, GE)
         tt(R("vi", hh[0], hh[1], rows=nl), R("sc" + X, 15, 128, 16, rows=nl), R("sf" + X, rows=nl), MAX)
         ts(R("id%d" % (hop % 2), hh[0], hh[1], rows=nl), R("vi", hh[0], hh[1], rows=nl), 8191, None, AND)
         if hop < H:
             tt(R("xx", 128 * h, 128 * h + 128), R("id%d" % (hop % 2), hh[0], hh[1]), R("mask", 0, 128), MUL, ind=R("rep", 0, 8))
-            mm(R("bp" + X, 128, 128 + st["nc"]), R("xx", 128 * h, 128 * h + 128, rows=nl), R("cm", 0, st["nc"], rows=nl), True, True)
+            mm(R(acc, 400, 400 + st["nc"]), R("xx", 128 * h, 128 * h + 128, rows=nl), R("cm", 0, st["nc"], rows=nl), True, True)
 
     def nextlist(st):
-        X, h, nl, hop, nc = st["X"], st["h"], st["nl"], st["hop"], st["nc"]
-        tc(R("l" + X, 0, nc), R("bp" + X, 128, 128 + nc))
+        X, hop, nc = st["X"], st["hop"], st["nc"]
+        tc(R("l" + X, 0, nc), R("acc" + X, 400, 400 + nc))
         st["list"] = R("l" + X, 0, nc)
         nbg(st)
-        ts(R("idp", 8 * h, 8 * h + 8, rows=nl), R("id%d" % (hop % 2), 8 * h, 8 * h + 8, rows=nl), float(-OFS), None, ADD)
         if hop == H - 1:
-            tc(R("sL", st["c0"], st["c0"] + nc), R("bp" + X, 128, 128 + nc))
+            tc(R("sL", st["c0"], st["c0"] + nc), R("acc" + X, 400, 400 + nc))
         st["hop"] = hop + 1
 
     def places(t, sts):
@@ -594,7 +598,7 @@ def rank_program(g, core, T, topo):
     def landed(t):
         for e in range(1, 8):
             o, i = R("f", OWN + S + (e - 1) * G, OWN + S + e * G), R("ld%d" % t, (7 - e) * BW, (7 - e) * BW + G)
-            if e in (2, 5):
+            if e in (2, 4, 6):
                 act(o, i, COPY)
             else:
                 tc(o, i)
@@ -619,7 +623,7 @@ def rank_program(g, core, T, topo):
             agat(X, 0)
             if slot == 0:
                 start(Y)
-                maxes(X, 0, range(NV))
+                maxes(X, 0, range(NC))
             else:
                 tail(Y)
                 maxes(X, 0, range(0, K1))
@@ -627,12 +631,12 @@ def rank_program(g, core, T, topo):
                     places(t, sts)
                 else:
                     nextlist(Y)
-                maxes(X, 0, range(K1, NV))
+                maxes(X, 0, range(K1, NC))
             agat(X, 1)
             amm(X)
             if last:
                 places2(t, sts)
-            maxes(X, 1, range(NV))
+            maxes(X, 1, range(NC))
         places3(t, sts)
         tail(order[1])
         moves(t, sts)

from concourse.bass import DstId, RemoteDMATransfer
from concourse.mybir import dt, AluOpType, AxisListType, ActivationFunctionType

ADD, SUB, MUL, MAX, MIN = AluOpType.add, AluOpType.subtract, AluOpType.mult, AluOpType.max, AluOpType.min
GE, GT, LE, LT, EQ = AluOpType.is_ge, AluOpType.is_gt, AluOpType.is_le, AluOpType.is_lt, AluOpType.is_equal
SHR, AND = AluOpType.arith_shift_right, AluOpType.bitwise_and
IDEN, COPY = ActivationFunctionType.Identity, ActivationFunctionType.Copy

N, S, G, CAP, WN, M, RO, H, T0 = 8, 3328, 112, 16, 144, 512, 3, 4, 192
OWN = 512
NULL = S + (N - 1) * G
FW = OWN + NULL + 16
BW = 120
K17 = 17 * 8192
OFS = 99 * K17
NV = 16
RR = 4
NC = NV // RR
MAGIC = 12582912.0
K1 = 2

SCRATCH = {}
for _n, _w, _t in (
        ("f", FW, "bfloat16"), ("nbw", NULL + 16, "int32"), ("pl", M, "bfloat16"), ("wti", 1, "int32"), ("wni", 27, "int32"), ("sdi", 49, "int32"),
        ("sdp", 56, "uint16"), ("sdf", 56, "float32"), ("sdw", 800, "float32"), ("sdx", 784, "float32"), ("wl", 30, "uint16"), ("rep", 50, "uint16"),
        ("wq", 432, "float32"), ("jf", 128, "float32"), ("jmf", 256, "float32"), ("j4", 128, "float32"), ("j7", 128, "float32"), ("j3", 64, "float32"),
        ("ji", 64, "int32"), ("cols", 40, "float32"), ("idf", 128, "float32"), ("idh", 128, "float16"), ("idb", 128, "bfloat16"),
        ("mask", 256, "float32"), ("rep8", 8, "uint16"), ("rep87", 16, "uint16"), ("blk", 128, "float32"), ("wm", 24, "bfloat16"),
        ("wa", 24, "bfloat16"), ("wb", 264, "bfloat16"), ("wz", 8, "bfloat16"), ("ws", 8, "bfloat16"), ("rsm", 128, "float32"), ("rsa", 112, "float32"),
        ("rs8", 128, "float32"), ("tril", 128, "bfloat16"), ("ones", 128, "bfloat16"), ("k9", 8, "bfloat16"), ("ec", 128, "float32"), ("onf", 128, "float32"),
        ("gm", 64, "float32"), ("b", 256, "bfloat16"), ("xx", 256, "float32"), ("dx", 256, "float32"), ("dl", 16, "uint16"), ("dlm", 16, "uint16"),
        ("fd", 256, "bfloat16"), ("uu", 256, "bfloat16"), ("uv", 256, "float32"), ("val", 512, "bfloat16"), ("ex", 256, "float16"), ("da", 256, "float16"),
        ("trash", 256, "bfloat16"), ("ofl", 32, "uint16"), ("on", 128, "bfloat16"), ("qb", 128, "float32"), ("qs", 128, "float32"),
        ("mh", 256, "bfloat16"), ("ek", 128, "bfloat16"), ("rq", 64, "float32"), ("gg", 7 * BW, "bfloat16"), ("ld0", 7 * BW, "bfloat16"),
        ("ld1", 7 * BW, "bfloat16"), ("ld2", 7 * BW, "bfloat16"), ("rki", 8, "uint16"), ("qa", 128, "float32"), ("qc", 128, "float32")):
    SCRATCH[_n] = ("sbuf", [128, _w], _t)
for _x in "AB":
    for _n, _w, _t in (("l", 8, "uint16"), ("off", 128, "uint16"), ("a", 2048, "bfloat16"), ("m", 2048, "bfloat16"), ("cp", 128, "float32"),
                       ("t1", 128, "float32"), ("u", 128, "float32"), ("k", 128, "float32"), ("sc", 128, "float32")):
        SCRATCH[_n + _x] = ("sbuf", [128, _w], _t)
for _n, _t in (("jm3", "float32"), ("dg", "bfloat16"), ("dgs", "float32"), ("trw", "float32"), ("tru", "float32")):
    SCRATCH[_n] = ("sbuf", [128, 16, 16], _t)
SCRATCH["e3"] = ("sbuf", [128, 16, 272], "bfloat16")
for _n in ("accA", "accB", "bpA", "bpB", "q1", "q2", "q3"):
    SCRATCH[_n] = ("psum", [128, 512], "float32")
SCRATCH["tri3"] = ("psum", [128, 16, 16], "float32")
PSUMS = [k for k in SCRATCH if SCRATCH[k][0] == "psum"]
ALIAS = {}
for _buf, _t, _names in (
        ("tf", "float32", (("sL", 16), ("idp", 16), ("alive", 16), ("dT", 16), ("em", 16), ("dmu", 16), ("dc", 16), ("cnt", 16), ("eb", 16), ("kq", 16), ("se", 16),
                           ("ucode", 16), ("uc2", 16), ("dLc", 16), ("c113", 8), ("rk", 8), ("cm", 8), ("sfA", 8), ("sfB", 8), ("fl", 16), ("base", 32),
                           ("basm", 32), ("w2", 32), ("of", 32), ("a12", 32), ("wf", 32))),
        ("ti", "int32", (("vi", 16), ("id0", 16), ("id1", 16), ("zi", 16), ("zm", 16), ("zq", 16), ("zh", 16), ("zg", 16), ("dLi", 16), ("dLm", 16),
                         ("ebi", 16), ("rpi", 8), ("ci", 8)))):
    _o = 0
    for _n, _w in _names:
        ALIAS[_n] = (_buf, _o, _w)
        _o += _w
    SCRATCH[_buf] = ("sbuf", [128, _o], _t)
SEMAPHORES = ["sv", "ss", "sp", "sg"] + ["d%d" % i for i in range(12)] + ["arr0", "arr1", "arr2"] + ["snd%d" % i for i in range(9)]


def R(name, lo=None, hi=None, step=None, rows=128, extra=None):
    if name in ALIAS:
        buf, o, w = ALIAS[name]
        return (buf, o + (0 if lo is None else lo), o + (w if hi is None else hi), step, rows, extra)
    return (name, lo, hi, step, rows, extra)


def rank_program(g, core, T, topo):
    rank = T.rank_of(core)
    if rank is None:
        return
    qs = {"v": g.vector, "s": g.scalar, "p": g.tensor, "g": g, "y": g.sync}
    semof = {"v": "sv", "s": "ss", "p": "sp", "g": "sg"}
    cnt = {"v": 0, "s": 0, "p": 0, "g": 0}
    known = {"v": {}, "s": {}, "p": {}, "g": {}, "y": {}}
    hist = {}
    dman = [0]
    sent = {}

    def ap(r):
        name, lo, hi, step, rows, extra = r
        t = T[name]
        if extra is not None:
            return t[(slice(0, rows),) + extra]
        if lo is None:
            return t[:] if rows == 128 else t[0:rows]
        return t[0:rows, lo:hi] if step is None else t[0:rows, lo:hi:step]

    def span(r):
        name, lo, hi, step, rows, extra = r
        if extra is not None and not isinstance(extra[0], slice):
            return name, 1000 * extra[0], 1000 * extra[0] + 1000
        if name in PSUMS or lo is None:
            return name, 0, 1 << 20
        return name, lo, hi

    def emit(q, fn, reads, writes, sem=None, inc=1, dma=False):
        acc = [(span(r), False) for r in reads] + [(span(r), True) for r in writes]
        deps = []
        for (name, lo, hi), w in acc:
            for rec in hist.get(name, ()):
                if rec[1] <= lo or rec[0] >= hi:
                    continue
                same = rec[3] == q and not dma and not rec[7]
                if same and name in PSUMS and q == "p":
                    need = False
                elif name in PSUMS and not same:
                    need = True
                else:
                    need = rec[2] or w
                if need:
                    deps.append(rec)
        deps.sort(key=lambda rec: -len(rec[6]) * 100000 - rec[5])
        kn = known[q]
        for rec in deps:
            if kn.get(rec[4], 0) >= rec[5]:
                continue
            val = rec[5]
            for o in deps:
                if o[4] == rec[4]:
                    val = max(val, o[5])
            qs[q].wait_ge(T.sem[rec[4]], val)
            kn[rec[4]] = val
            for o in deps:
                if o[4] == rec[4] and o[5] <= val:
                    for k, v in o[6].items():
                        if kn.get(k, 0) < v:
                            kn[k] = v
        ins = fn()
        if sem is None:
            sem = semof[q]
            cnt[q] += 1
            val = cnt[q]
            ins.then_inc(T.sem[sem], 1)
        else:
            val = inc
        snap = dict(kn)
        snap[sem] = val
        for (name, lo, hi), w in acc:
            lst = hist.get(name, [])
            if w:
                lst = [rec for rec in lst if not (rec[0] >= lo and rec[1] <= hi)]
            else:
                lst = [rec for rec in lst if not (not rec[2] and rec[3] == q and rec[4] == sem and rec[0] >= lo and rec[1] <= hi)]
            lst.append((lo, hi, w, q, sem, val, snap, dma))
            hist[name] = lst
        return ins

    def dma(q, out, in_, outr, inr):
        sem = "d%d" % dman[0]
        dman[0] += 1
        emit(q, lambda: qs[q].dma_start(out, in_).then_inc(T.sem[sem], 16), inr, outr, sem=sem, inc=16, dma=True)

    def ts(out, in0, s1, s2, o0, o1=None, ind=None):
        rd = [in0] + [x for x in (s1, s2, ind) if isinstance(x, tuple)]
        a1 = ap(s1) if isinstance(s1, tuple) else s1
        a2 = ap(s2) if isinstance(s2, tuple) else s2
        i0 = ap(in0).indirect(ap(ind)) if ind else ap(in0)
        if o1 is None:
            emit("v", lambda: g.vector.tensor_scalar(ap(out), i0, a1, None, o0), rd, [out])
        else:
            emit("v", lambda: g.vector.tensor_scalar(ap(out), i0, a1, a2, o0, o1), rd, [out])

    def tt(out, in0, in1, op, ind=None):
        i0 = ap(in0).indirect(ap(ind)) if ind else ap(in0)
        emit("v", lambda: g.vector.tensor_tensor(ap(out), i0, ap(in1), op), [in0, in1] + ([ind] if ind else []), [out])

    def tc(out, in_, ind=None, oind=None):
        i0 = ap(in_).indirect(ap(ind)) if ind else ap(in_)
        o = ap(out).indirect(ap(oind)) if oind else ap(out)
        emit("v", lambda: g.vector.tensor_copy(o, i0), [in_] + ([ind] if ind else []) + ([oind] if oind else []), [out])

    def scan(out, d0, d1, init, o0, o1):
        emit("v", lambda: g.vector.tensor_tensor_scan(ap(out), ap(d0), ap(d1), init, o0, o1), [d0, d1], [out])

    def ms(out, c):
        emit("v", lambda: g.vector.memset(ap(out), c), [], [out])

    def act(out, in_, func, bias=None, scale=None, ind=None, accum=None):
        i0 = ap(in_).indirect(ap(ind)) if ind else ap(in_)
        kw = {}
        rd = [in_] + ([ind] if ind else [])
        wr = [out]
        if bias is not None:
            kw["bias"] = ap(bias)
            rd.append(bias)
        if scale is not None:
            kw["scale"] = ap(scale)
            rd.append(scale)
        if accum is not None:
            kw["accum_out"] = ap(accum)
            wr.append(accum)
        emit("s", lambda: g.scalar.activation(ap(out), i0, func, **kw), rd, wr)

    def mm(out, lhsT, rhs, start, stop):
        emit("p", lambda: g.tensor.matmul(ap(out), ap(lhsT), ap(rhs), start, stop), [lhsT, rhs], [out])

    def iota(out, pattern, base, cmul, flt=True):
        if flt:
            emit("g", lambda: g.iota(ap(out), pattern, base, cmul, allow_small_or_imprecise_dtypes=True), [], [out])
        else:
            emit("g", lambda: g.iota(ap(out), pattern, base, cmul), [], [out])

    COL = {}

    def col(name):
        if name not in COL:
            COL[name] = len(COL)
        return R("cols", COL[name], COL[name] + 1)

    hx = S // 2
    dma("y", T.sdi[:], T.snd[:], [R("sdi")], [])
    dma("s", T.f[:, OWN + hx:OWN + S], T.x0[:, hx:S], [R("f", OWN + hx, OWN + S)], [])
    dma("y", T.f[:, OWN:OWN + hx], T.x0[:, 0:hx], [R("f", OWN, OWN + hx)], [])
    dma("s", T.wti[:], T.wt[:], [R("wti")], [])
    dma("y", T.wni[:], T.wants[:], [R("wni")], [])
    dma("s", T.nbw[:, hx:S], T.nb[:, hx:S], [R("nbw", hx, S)], [])
    dma("y", T.nbw[:, 0:hx], T.nb[:, 0:hx], [R("nbw", 0, hx)], [])
    dma("y", T.pl[:], T.pull[:], [R("pl")], [])

    iota(R("ci", 0, 1), [[0, 1]], 0, 1, False)
    iota(R("jf"), [[1, 128]], 0, 0)
    iota(R("jmf"), [[0, 16], [1, 16]], 0, 0)
    iota(R("j4"), [[1, 8], [0, 16]], 0, 0)
    iota(R("ji"), [[1, 64]], 0, 0, False)
    iota(R("nbw", S, NULL + 1), [[1, NULL + 1 - S]], S, 0, False)

    ms(R("gg"), 0.0)
    for nm in ("id0", "id1"):
        ms(R(nm), 0)
    ms(R("alive"), 0.0)
    ms(R("cnt"), 0.0)
    ms(R("q1", 0, 64), 0.0)
    ms(R("q3", 0, 128), 0.0)
    ms(R("f", OWN + NULL, FW), -1.0)
    ms(R("ones"), 1.0)
    ms(R("k9"), -11.0 * K17)
    ms(R("wm", 0, 8), 0.0)
    ms(R("wa", 16, 24), 0.0)
    ts(R("ci", 1, 2), R("ci", 0, 1), 15, None, AND)
    ts(R("ci", 2, 3), R("ci", 0, 1), 4, None, SHR)
    tc(col("p"), R("ci", 0, 1))
    tc(col("q"), R("ci", 1, 2))
    tc(col("g"), R("ci", 2, 3))
    ts(R("ci", 3, 4), R("ci", 1, 2), 3, None, SHR)
    for e in range(7):
        tc(R("sdp", 8 * e, 8 * e + 7), R("sdi", 7 * e, 7 * e + 7))
    P34, P26 = float(2 ** 34), float(2 ** 26)
    ts(col("r15"), col("q"), 15.0, None, EQ)
    ts(col("rl"), col("q"), 15.0, None, LT)
    ts(col("b2"), col("r15"), 2.0, None, MUL)
    ts(col("nb"), col("q"), -8192.0, -8192.0 - OFS, MUL, ADD)
    ts(col("k17"), col("r15"), float(K17), None, MUL)
    ts(col("t34"), col("rl"), P34, None, MUL)
    ts(col("m34"), col("rl"), -P34, None, MUL)
    ts(col("m26"), col("r15"), -P26, None, MUL)
    tt(col("mt2"), col("m34"), col("m26"), ADD)
    ts(R("cm"), R("jf", 0, 8), col("g"), None, EQ)
    ts(R("idf"), R("jf"), col("p"), None, EQ)
    ts(R("blk"), R("j4"), col("g"), None, EQ)
    act(R("idb"), R("idf"), COPY)
    for k in (1, 2):
        act(R("wm", 8 * k, 8 * k + 8), R("cm"), COPY, scale=col("t34"))
    act(R("wa", 0, 8), R("cm"), COPY, scale=col("k17"))
    act(R("wa", 8, 16), R("cm"), COPY, scale=col("m34"))
    act(R("wb", 0, 128), R("blk"), COPY, scale=col("m26"))
    act(R("wb", 128, 256), R("blk"), COPY, scale=col("mt2"))
    act(R("wb", 256, 264), R("cm"), COPY, scale=col("k17"))
    act(R("ws"), R("cm"), COPY, scale=col("r15"))
    ts(R("mask"), R("jmf"), col("q"), None, EQ)
    ts(R("rsm"), R("jmf", 0, 128), 0.0, -1e29, EQ, MUL)

    off = [e for e in range(1, 8) if topo.chip(T.cores[(rank + e) % N]) != topo.chip(core)]
    near = [e for e in range(1, 8) if e not in off]
    calls = [off[0:4], off[4:] + near]

    def ghosts(t):
        order = calls[0] + calls[1]
        for e in order:
            o, w, i = R("gg", (e - 1) * BW, (e - 1) * BW + G), R("f", OWN, OWN + S), R("sdp", 8 * (e - 1), 8 * e - 1)
            if e == order[-1] or (t == 0 and e in order[-3:]):
                tc(o, w, ind=i)
            else:
                act(o, w, COPY, ind=i)

    def engines_of(src, es, e):
        me = T.cores[src]
        away = [x for x in es if topo.chip(T.cores[(src + x) % N]) != topo.chip(me)]
        out = {}
        used = []
        for x in away + [y for y in es if y not in away]:
            eng = topo.engines(me, T.cores[(src + x) % N])
            free = [y for y in eng if y not in used]
            room = len(eng) // len(away) if x in away else len(free)
            n = 1
            while n * 2 <= room:
                n *= 2
            out[x] = free[0:n]
            used = used + out[x]
        return out[e]

    def send(t):
        for k, es in enumerate(calls):
            trs = []
            inc = 0
            for e in es:
                dst = T.cores[(rank + e) % N]
                mine = engines_of(rank, es, e)
                rid, pid, se = topo.addr(dst)
                mk = 0
                for x in mine:
                    mk += 1 << x
                p = 7 - e
                trs.append(RemoteDMATransfer(dst_ids=[DstId(rid=rid, pnc=pid)], dma_engine_mask=mk, remote_sem=T.sem["arr%d" % t],
                                             srcs=[T.gg[:, (e - 1) * BW:e * BW]], dsts=[T["ld%d" % t][:, p * BW:(p + 1) * BW]]))
                inc += len(mine)
            sem = "snd%d" % (3 * t + k)
            emit("g", lambda: g.remote_dma_fused(trs, local_sem=T.sem[sem]), [R("gg", (e - 1) * BW, e * BW) for e in es], [], sem=sem, inc=inc, dma=True)
            sent[sem] = inc
        arrived = 0
        for e in range(1, 8):
            src = (rank - e) % N
            soff = [x for x in range(1, 8) if topo.chip(T.cores[(src + x) % N]) != topo.chip(T.cores[src])]
            snear = [x for x in range(1, 8) if x not in soff]
            arrived += len(engines_of(src, soff[0:4] if e in soff[0:4] else soff[4:] + snear, e))
        hist["ld%d" % t] = [(0, 1 << 20, True, "r", "arr%d" % t, arrived, {}, True)]

    ghosts(0)
    send(0)
    iota(R("j7"), [[0, 16], [1, 8]], 0, 0)
    iota(R("j3"), [[1, 8], [0, 8]], 0, 0)
    iota(R("jm3"), [[0, 16], [1, 16]], 0, 0)
    iota(R("c113"), [[113, 8]], 0, 0)

    tc(R("rep"), R("ji", 0, 50))
    tc(R("wl", 0, 9), R("wni", 0, 9))
    ms(R("wf"), 0.0)
    tc(R("wf", 0, 27), R("wni"))
    tt(R("wq", 0, 144), R("wf", 0, 32), R("mask", 0, 144), MUL, ind=R("rep", 0, 9))

    def setup_hops():
        tc(col("wt"), R("wti"))
        tt(col("wtl"), col("wt"), col("rl"), MUL)
        act(R("wz"), R("cm"), COPY, scale=col("wtl"))
        ts(col("neg"), col("r15"), -1.0, None, MUL)
        ts(col("half"), col("rl"), 0.5, None, MUL)
        ts(col("q0"), col("rl"), -0.25, None, MUL)
        for t in range(RO):
            ts(col("st%d" % t), col("r15"), float(T0 + t), None, MUL)
            tt(col("nb%d" % t), col("st%d" % t), col("q0"), ADD)
        for t in (1, 2):
            tc(R("wl", 10 * t + 1, 10 * t + 10), R("wni", 9 * t, 9 * t + 9))
        tc(R("idh"), R("idf"))
        ts(R("rs8"), R("j7"), 0.0, None, GT)
        ts(R("ec"), R("j7"), -1.0, 7.0, MUL, ADD)
        ts(R("onf"), R("j7"), 7.0, 99.0, EQ, MUL)
        tt(R("ec"), R("ec"), R("onf"), ADD)
        ts(R("tril"), R("jf"), col("p"), None, GT)
        ts(R("gm"), R("j3"), col("g"), None, EQ)
        ts(R("trw"), R("jm3"), col("q"), 1.5, LT, MUL)
        ts(R("tru"), R("jm3"), col("q"), -0.5, LE, MUL)
        tt(R("tri3"), R("trw"), R("tru"), ADD)
        ts(R("base"), R("jf", 0, 32), 16.0, col("q"), MUL, ADD)
        ts(R("basm"), R("base"), float(-OWN), None, ADD)
        for h in (0, 1):
            ts(R("ucode", 8 * h, 8 * h + 8), R("jf", 0, 8), 0.0, float(S - 2048 + 128 * h), MUL, ADD)
        ts(R("ucode"), R("ucode"), col("p"), None, ADD)
        ts(R("uc2"), R("ucode"), 2048.0, None, ADD)
        tc(col("q8"), R("ci", 3, 4))
        ts(R("rk"), R("jf", 0, 8), 2.0, col("q8"), MUL, ADD)
        tc(R("rep8"), R("rk"))
        ts(R("zi"), R("ji", 0, 16), 8.0, 7.0, MUL, ADD)
        tc(R("rep87"), R("zi"))

    def setup_later():
        for t in (1, 2):
            w0 = 8 * ((9 * t) // 8)
            for lo, n in ((0, 8), (8, 1)):
                ts(R("rpi", 0, n), R("ji", 0, n), float(9 * t - w0 + lo), None, ADD)
                tc(R("rki", 0, n), R("rpi", 0, n))
                tt(R("wq", 144 * t + 16 * lo, 144 * t + 16 * lo + 16 * n), R("wf", w0, 32), R("mask", 0, 16 * n), MUL, ind=R("rki", 0, n))
        tc(R("sdf", 0, 49), R("sdi"))
        ms(R("sdf", 49, 56), 0.0)
        for lo in range(0, 49, 16):
            hi = min(49, lo + 16)
            tt(R("sdx", 16 * lo, 16 * hi), R("sdf"), R("mask", 0, 16 * (hi - lo)), MUL, ind=R("rep", lo, hi))
        ms(R("sdw", 0, 784, 113), float(NULL))
        ts(R("rsa"), R("jmf", 0, 112), 0.0, None, GT)
        for lo, hi in ((0, 4 * G), (4 * G, 7 * G)):
            mm(R("q2", 0, hi - lo), R("blk"), R("sdx", lo, hi), True, True)
            for e in range(lo // G, hi // G):
                act(R("sdw", 113 * e + 1, 113 * e + 113), R("q2", e * G - lo, (e + 1) * G - lo), COPY)

    def stream(X, t):
        h = 0 if X == "A" else 1
        nc = (4, 5)[h] if t == 0 else 8
        c0 = 0 if h == 0 else (4 if t == 0 else 8)
        return {"X": X, "h": h, "nl": 16 * nc, "nc": nc, "c0": c0, "l0": 16 * c0, "hop": 1, "t": t}

    def start(st):
        X, t, h, nl = st["X"], st["t"], st["h"], st["nl"]
        if t == 0:
            st["list"] = R("wl", st["c0"], st["c0"] + st["nc"])
            src = R("wq", st["l0"], st["l0"] + nl)
        elif h == 1:
            st["list"] = R("wl", 10 * t + 2, 10 * t + 10)
            src = R("wq", 144 * t + 16, 144 * t + 144)
        else:
            tt(R("rk", 0, 7), R("ld%d" % t, G, 7 * BW, BW), R("c113", 0, 7), ADD)
            tc(R("rki", 0, 7), R("rk", 0, 7))
            tt(R("qa", 0, 112), R("sdw", 0, 791), R("mask", 0, 112), MUL, ind=R("rki", 0, 7))
            tc(R("lA", 7, 8), R("wl", 10 * t + 1, 10 * t + 2))
            scan(R("qc", 0, 112), R("rsa"), R("qa", 0, 112), 0.0, MUL, ADD)
            tc(R("lA", 0, 7), R("qc", 15, 112, 16))
            act(R("qa", 112, 128), R("wq", 144 * t, 144 * t + 16), COPY)
            st["list"] = R("lA")
            src = R("qa")
        mm(R("acc" + X, 408, 416, rows=nl), src, R("cm"), True, True)
        nbg(st)
        tc(R("idp", 8 * h, 8 * h + 8, rows=nl), R("acc" + X, 408, 416, rows=nl))

    def nbg(st):
        X, nl = st["X"], st["nl"]
        tc(R("off" + X, 0, nl), R("nbw"), ind=st["list"])

    def compv(st):
        X, nl = st["X"], st["nl"]
        ts(R("cp" + X, 0, nl), R("off" + X, 0, nl), col("nb"), None, ADD)

    def bgat(st):
        X, h, nl, l0 = st["X"], st["h"], st["nl"], st["l0"]
        bb = R("b", l0, l0 + nl)
        ts(bb, R("f", OWN, FW), col("b2"), None, ADD, ind=st["list"])
        for j in range(RR):
            mm(R("bp" + X, j, RR * nl, RR), R("idb"), bb, True, True)
        mm(R("acc" + X, 128, 392, rows=nl), bb, R("wb"), True, False)
        mm(R("acc" + X, 384, 392, rows=nl), R("ones", 0, nl, rows=9), R("k9", rows=9), False, False)
        mm(R("acc" + X, 0, 128, rows=nl), R("cp" + X, 0, nl), R("idf"), False, False)
        if st["hop"] == H:
            mm(R("q1", 8 * h, 8 * h + 8, rows=nl), bb, R("wz"), True, True)

    def chunk(st, k):
        n2 = 64 if st["nl"] == 128 else 32
        return (0, n2) if k == 0 else (n2, st["nl"])

    def agat(st, k):
        X = st["X"]
        lo, hi = chunk(st, k)
        act(R("a" + X, 16 * lo, 16 * hi), R("f", OWN, FW), IDEN, bias=col("b2"), ind=R("off" + X, lo, hi))

    def amm(st):
        X, nl = st["X"], st["nl"]
        for n in range(NV):
            mm(R("acc" + X, n, 384, 16, rows=nl), R("a" + X, n, 16 * nl, 16), R("wa"), False, False)

    def maxes(st, k, ns):
        X, nl = st["X"], st["nl"]
        lo, hi = chunk(st, k)
        for n in ns:
            tt(R("m" + X, RR * (n * nl + lo), RR * (n * nl + hi)), R("a" + X, 16 * lo + n, 16 * hi, NC), R("bp" + X, RR * lo, RR * hi), MAX)
            if k == 1:
                for j in range(RR):
                    mm(R("acc" + X, n + NC * j, 384, 16, rows=nl), R("m" + X, RR * n * nl + j, RR * (n + 1) * nl, RR), R("wm"), False,
                       n == NC - 1 and j == RR - 1)

    def tail(st):
        X, h, nl, hop = st["X"], st["h"], st["nl"], st["hop"]
        acc = "acc" + X
        hh = (8 * h, 8 * h + 8)
        tc(R("t1" + X, rows=nl), R(acc, 128, 256, rows=nl))
        tt(R("u" + X, rows=nl), R("t1" + X, rows=nl), R(acc, 256, 384, rows=nl), MIN)
        tt(R("k" + X, rows=nl), R("u" + X, rows=nl), R(acc, 0, 128, rows=nl), MIN)
        tt(R("sf" + X, rows=nl), R("idp" if hop == 1 else "id%d" % (1 - hop % 2), hh[0], hh[1], rows=nl), R(acc, 384, 392, rows=nl), ADD)
        scan(R("sc" + X, rows=nl), R("rsm", rows=nl), R("k" + X, rows=nl), -1e29, ADD, MAX)
        if hop == 1:
            ts(R("alive", hh[0], hh[1], rows=nl), R(acc, 384, 392, rows=nl), 1.5 * K17 - OFS, None, GE)
        tt(R("vi", hh[0], hh[1], rows=nl), R("sc" + X, 15, 128, 16, rows=nl), R("sf" + X, rows=nl), MAX)
        ts(R("id%d" % (hop % 2), hh[0], hh[1], rows=nl), R("vi", hh[0], hh[1], rows=nl), 8191, None, AND)
        if hop < H:
            tt(R("xx", 128 * h, 128 * h + 128), R("id%d" % (hop % 2), hh[0], hh[1]), R("mask", 0, 128), MUL, ind=R("rep", 0, 8))
            mm(R(acc, 400, 400 + st["nc"]), R("xx", 128 * h, 128 * h + 128, rows=nl), R("cm", 0, st["nc"], rows=nl), True, True)

    def nextlist(st):
        X, hop, nc = st["X"], st["hop"], st["nc"]
        tc(R("l" + X, 0, nc), R("acc" + X, 400, 400 + nc))
        st["list"] = R("l" + X, 0, nc)
        nbg(st)
        if hop == H - 1:
            tc(R("sL", st["c0"], st["c0"] + nc), R("acc" + X, 400, 400 + nc))
        st["hop"] = hop + 1

    def places(t, sts):
        tc(R("zi"), R("q1", 0, 16))
        ts(R("zm"), R("zi"), 4095, None, AND)
        tt(R("zq"), R("zm"), R("zm"), MUL)
        if t:
            ts(R("zi"), R("zq"), float(97 * 32 * t), None, ADD)
        ts(R("zh"), R("zi" if t else "zq"), 5, 4095, SHR, AND)
        ts(R("zg"), R("zh"), float(S), float(-S), GE, MUL)
        tt(R("dT"), R("zh"), R("zg"), ADD)
        tt(R("dx"), R("dT"), R("mask", 0, 256), MUL, ind=R("rep", 0, 16))
        for st in sts:
            mm(R("q1", 16 + st["c0"], 16 + st["c0"] + st["nc"]), R("dx", 128 * st["h"], 128 * st["h"] + 128, rows=st["nl"]),
               R("cm", 0, st["nc"], rows=st["nl"]), True, True)

    def places2(t, sts):
        nc = sum(st["nc"] for st in sts)
        L = 16 * nc
        tc(R("dLi", 0, nc), R("q1", 16, 16 + nc))
        tc(R("dl", 0, nc), R("dLi", 0, nc))
        act(R("fd", 0, L), R("f", OWN, OWN + S), COPY, ind=R("dl", 0, nc))
        ts(R("dLm", 0, nc), R("dLi", 0, nc), M - 1, None, AND)
        tc(R("dlm", 0, nc), R("dLm", 0, nc))
        act(R("uu", 0, L), R("pl"), COPY, ind=R("dlm", 0, nc))
        ts(R("dLc", 0, nc), R("dLi", 0, nc), -2048.0, None, ADD)
        tt(R("dmu"), R("dT"), R("uc2"), SUB)
        ts(R("se"), R("id1"), float(S), None, LT)
        tt(R("se"), R("se"), R("alive"), MUL)
        tt(R("dmu"), R("dmu"), R("se"), MUL)
        tt(R("a12", 0, nc), R("dLi", 0, nc), R("basm", 0, nc), SUB)
        tt(R("a12", nc, 2 * nc), R("sL", 0, nc), R("basm", nc, 2 * nc), SUB)

    def places3(t, sts):
        nc = sum(st["nc"] for st in sts)
        L = 16 * nc
        for st in sts:
            mm(R("q1", 32 + 8 * st["h"], 40 + 8 * st["h"], rows=st["nl"]), R("fd", st["l0"], st["l0"] + st["nl"]), R("ws"), True, True)
        mm(R("q2", 0, L), R("idb"), R("uu", 0, L), True, False)
        mm(R("q2", 0, L), R("idb"), R("b", 0, L), False, True)
        ts(R("em"), R("q1", 32, 48), 0.0, None, LT)
        tt(R("dmu"), R("em"), R("dmu"), MUL)

    def moves(t, sts):
        nc = sum(st["nc"] for st in sts)
        L = 16 * nc
        act(R("uv", 0, L), R("q2", 0, L), IDEN, bias=col("nb%d" % t), scale=col("half"))
        act(R("val", L, 2 * L), R("b", 0, L), IDEN, bias=col("neg"), scale=col("rl"))
        tt(R("se"), R("id0"), R("id1"), EQ)
        tt(R("dc"), R("se"), R("dmu"), MUL)
        tt(R("dc"), R("dc"), R("ucode"), ADD)
        tc(R("ex"), R("dc"), ind=R("rep", 0, 16))
        for st in sts:
            mm(R("q2", st["l0"], st["l0"] + st["nl"]), R("ex", 128 * st["h"], 128 * st["h"] + 128, rows=st["nl"]), R("idh", 0, st["nl"], rows=st["nl"]), True, True)
        ts(R("val", 0, L), R("uv", 0, L), MAGIC, -MAGIC, ADD, ADD)
        tc(R("da", 0, L), R("q2", 0, L))
        for c in range(nc - 1, -1, -1):
            ts(R("e3", extra=(c, slice(256 - 16 * c, 272))), R("da", 0, 16 * c + 16), R("dLc", c, c + 1), None, EQ)
            if c:
                act(R("trash", 0, 16 * c), R("e3", extra=(c, slice(256 - 16 * c, 256))), COPY, accum=R("cnt", c, c + 1))
        sl = slice(0, nc)
        tt(R("dg", extra=(sl, slice(0, 16))), R("e3", extra=(sl, slice(256, 272))), R("tri3", extra=(sl, slice(0, 16))), MUL)
        for w in (8, 4, 2, 1):
            src = "dg" if w == 8 else "dgs"
            tt(R("dgs", extra=(sl, slice(0, w))), R(src, extra=(sl, slice(0, w))), R(src, extra=(sl, slice(w, 2 * w))), ADD)

    def moves2(t, sts):
        nc = sum(st["nc"] for st in sts)
        L = 16 * nc
        tt(R("fl", 0, nc), R("cnt", 0, nc), R("dgs", extra=(slice(0, nc), 0)), ADD)
        for k in (0, nc):
            ts(R("w2", k, k + nc), R("fl", 0, nc), -0.25, None, LT)
        tt(R("of", 0, 2 * nc), R("w2", 0, 2 * nc), R("a12", 0, 2 * nc), MUL)
        tt(R("of", 0, 2 * nc), R("of", 0, 2 * nc), R("base", 0, 2 * nc), ADD)
        tc(R("ofl", 0, 2 * nc), R("of", 0, 2 * nc))
        tc(R("f", 0, OWN + S), R("val", 0, 2 * L), oind=R("ofl", 0, 2 * nc))

    def requests(sts, part):
        if part == 0:
            ts(R("ebi"), R("id0"), 1.0 / G, 1.0 - (S + (G - 1) / 2) / G, MUL, ADD)
            tt(R("eb"), R("ebi"), R("alive"), MUL)
            ts(R("kq"), R("ebi"), float(-G), float(-(S - G - 1)), MUL, ADD)
            tt(R("kq"), R("kq"), R("id0"), ADD)
            tt(R("on"), R("eb"), R("ec"), EQ, ind=R("rep8"))
            for st in sts:
                nl, h = st["nl"], st["h"]
                if h == 0:
                    mm(R("q3", 0, 64, rows=nl), R("tril", 0, nl, rows=nl), R("on", 0, 64, rows=nl), True, True)
                else:
                    n0 = sts[0]["nl"]
                    mm(R("q3", 64, 128, rows=nl), R("tril", 0, nl, rows=nl), R("on", 64, 128, rows=nl), True, False)
                    mm(R("q3", 64, 128, rows=nl), R("ones", 0, nl, rows=n0), R("on", 0, 64, rows=n0), False, True)
        elif part == 1:
            tt(R("qb"), R("on"), R("q3", 0, 128), MUL)
            scan(R("qs"), R("rs8"), R("qb"), 0.0, MUL, ADD)
            tt(R("mh"), R("qs"), R("jmf"), EQ, ind=R("rep87"))
            tt(R("ek"), R("kq"), R("on"), MUL, ind=R("rep8"))
            for st in sts:
                nl, h = st["nl"], st["h"]
                mm(R("q3", 128, 192), R("mh", 128 * h, 128 * h + 128, rows=nl), R("ek", 64 * h, 64 * h + 64, rows=nl), h == 0, h == 1)
        else:
            tt(R("rq"), R("gm"), R("q3", 128, 192), MUL)
            tt(R("rq", 0, 32), R("rq", 0, 32), R("rq", 32, 64), ADD)
            tt(R("rq", 0, 16), R("rq", 0, 16), R("rq", 16, 32), ADD)
            tt(R("gg", G, 7 * BW, BW), R("rq", 0, 7), R("rq", 8, 15), ADD)

    def landed(t):
        for e in range(1, 8):
            o, i = R("f", OWN + S + (e - 1) * G, OWN + S + e * G), R("ld%d" % t, (7 - e) * BW, (7 - e) * BW + G)
            if e in (2, 4, 6):
                act(o, i, COPY)
            else:
                tc(o, i)

    for t in range(RO):
        A, B = stream("A", t), stream("B", t)
        sts = (A, B)
        order = (A, B) if t == 0 else (B, A)
        if t == 1:
            setup_later()
        start(order[0])
        compv(order[0])
        if t == 0:
            setup_hops()
        landed(t)
        for slot in range(2 * H):
            X, Y = order[slot % 2], order[1 - slot % 2]
            last = slot == 2 * H - 1
            if slot:
                compv(X)
            bgat(X)
            agat(X, 0)
            if slot == 0:
                start(Y)
                maxes(X, 0, range(NC))
            else:
                tail(Y)
                maxes(X, 0, range(0, K1))
                if last:
                    places(t, sts)
                else:
                    nextlist(Y)
                maxes(X, 0, range(K1, NC))
            agat(X, 1)
            amm(X)
            if last:
                places2(t, sts)
            maxes(X, 1, range(NC))
        places3(t, sts)
        tail(order[1])
        moves(t, sts)
        if t + 1 < RO:
            requests(sts, 0)
        moves2(t, sts)
        if t + 1 < RO:
            requests(sts, 1)
            ghosts(t + 1)
            requests(sts, 2)
            send(t + 1)
    emit("y", lambda: g.sync.dma_start(T.y[:], T.f[:, OWN:OWN + S]).then_inc(T.sem["d11"], 16), [R("f", OWN, OWN + S)], [], sem="d11", inc=16, dma=True)
    g.sync.wait_ge(T.sem["d11"], 16)
    for q in ("v", "s", "p", "g"):
        g.wait_ge(T.sem[semof[q]], cnt[q])
    for name, val in sorted(sent.items()):
        g.wait_ge(T.sem[name], val)
    for i in range(dman[0]):
        g.wait_ge(T.sem["d%d" % i], 16)
